import numpy as np, ml_dtypes
CORES = [16,17,18,19,32,33,34,35]
N = 8
import mx_ref
BF = ml_dtypes.bfloat16
def pick(q, e):
    c = np.concatenate([q[0].reshape(128, -1, 4), np.zeros((128, 1, 4), np.uint8)], axis=1); s = np.concatenate([q[1], np.ones((16, 1), np.uint8)], axis=1)
    return (np.ascontiguousarray(c[:, e].reshape(128, -1)), np.ascontiguousarray(s[:, e]))
def join(*qs):
    return (np.concatenate([q[0] for q in qs], axis=1), np.concatenate([q[1] for q in qs], axis=1))
def put(q, e, v):
    c, s = q[0].reshape(128, -1, 4).copy(), q[1].copy(); c[:, e] = v[0].reshape(128, -1, 4); s[:, e] = v[1]
    return (c.reshape(128, -1), s)
def pk(c, s):
    return (np.ascontiguousarray(c), mx_ref.live(s))
def emit(q):
    return q[0], q[1]
def tile(rs):
    return np.stack(rs, axis=2).reshape(128, -1).astype(BF)
def cut(t, i, w=512):
    return t[:, w * i:w * i + w]
def f(rng, *shape):
    return mx_ref.flush((rng.standard_normal(shape, dtype=np.float32) * np.exp2(rng.integers(-2, 3, shape[:-1] + (1,)))).astype(BF))
def wide(rng, *shape, cols=0):
    v = rng.standard_normal(shape, dtype=np.float32) * np.exp2(rng.integers(-12, 13, shape)).astype(np.float32)
    if cols: v *= np.repeat(np.exp2(rng.integers(-cols, cols + 1, shape[:-2] + (1, shape[-1] // 4))) * (rng.random(shape[:-2] + (1, shape[-1] // 4)) > 0.0625), 4, axis=-1).astype(np.float32)
    return mx_ref.flush(v.astype(BF))
P, CAPP, L, CB = 256, 64, 3, 64
def big(v, k):
    v = v.astype(np.float32) * np.float32(k)
    v[np.abs(v) < np.float32(2.0 ** -10)] = 0
    return v.astype(BF)
def number(z):
    n = np.zeros(z.shape[1], np.int64)
    for b in range(L): n += (z[b] < 0) * (1 << b)
    return n
def buckets(x, pl):
    X = [mx_ref.quantize(np.ascontiguousarray(x[s])) for s in range(N)]
    return X, np.stack([number(mx_ref.matmul(mx_ref.quantize(np.ascontiguousarray(pl[s])), X[s])) for s in range(N)])
def taken(bk):
    at = np.full((N, N, CAPP), -1)
    for d in range(N):
        for s in range(N):
            e = np.flatnonzero(bk[s] == d)[:CAPP]
            at[d, s, :e.size] = e
    return at
def attend(c, wv, e):
    e = np.concatenate([e, np.setdiff1d(np.arange(512), e)[:max(4 - len(e), len(e) % 2)]])
    m = pick(c, e)
    ct = [pick(c, np.arange(t, 512, 4)) for t in range(4)]
    A = tile([np.float32(0.0625) * np.maximum(mx_ref.matmul(k, m) + np.float32(0), np.float32(0)) for k in ct])
    qw = mx_ref.quantize(np.ascontiguousarray(wv))
    V = tile([mx_ref.matmul(k, qw) for k in ct])
    qa = mx_ref.quantize(A)
    O = [mx_ref.matmul(mx_ref.quantize(np.ascontiguousarray(cut(V, i))), qa) for i in range(4)]
    h = np.zeros((128, 512, 4), BF)
    h[:, e] = tile([np.float32(0.0625) * o for o in O]).reshape(128, -1, 4)
    return A, V, h.reshape(128, 2048)
def planes(rng):
    p = np.array(f(rng, 128, 512))
    p[:, 4 * L:] = 0
    return np.stack([p] * N)
def plain(rng):
    return {"x": big(f(rng, N, 128, 4 * P), 0.25), "pl": planes(rng), "p2": planes(rng), "wv": big(f(rng, N, 128, 2048), 0.25), "w": f(rng, N, 128, 512)}
def aimed(rng, d, want, gone=0, then=None, two=None):
    x, p = d["x"].astype(np.float32).reshape(N, 128, P, 4), np.zeros((128, 128, 4), np.float32)
    gone = np.zeros((N, P), np.int64) + gone
    at = rng.permutation(128)[:16 * L + 16].reshape(L + 1, 16)
    side = np.zeros((N, 128, 4), np.float32)
    for b in range(L):
        v = (1 + rng.random((16, 4))) * rng.choice([-1.0, 1.0], (16, 4))
        p[at[b], b] = v
        turn = (1 - 2 * (want >> b & 1)) * (1 - (gone >> b & 1))
        x[:, at[b]] = np.abs(x[:, at[b]]) * (np.sign(v)[None, :, None, :] * turn[:, None, :, None]) * (0.0625 if then is None else 1.0)
        side[:, at[b]] = np.sign(v)[None] * (1 - 2 * (np.arange(N) >> b & 1))[:, None, None]
    parted = np.zeros((128, 4), np.float32)
    if two is not None:
        k = two[2][:, None, :, None]
        u = rng.choice([-1.0, 1.0], (16, 4))
        parted[at[L]] = u
        x = np.where(k != 0, np.float32(0.125) * x, x)
        x[:, at[L]] = np.where(k != 0, 0.5 * (1 + rng.random((N, 16, P, 4))) * u[None, :, None, :] * k, x[:, at[L]])
    x = x * (gone != N - 1)[:, None, :, None]
    d = {**d, "x": big(x.reshape(N, 128, 4 * P), 1), "pl": np.stack([p.reshape(128, 512).astype(BF)] * N)}
    if then is None: return d
    p2, wv = np.zeros((128, 128, 4), np.float32), d["wv"].astype(np.float32).reshape(N, 128, 4, 128, 4)
    on = rng.permutation(128)[:16 * L].reshape(L, 16)
    for b in range(L):
        p2[on[b], b] = 1 + rng.random((16, 4))
        for q in range(N):
            sign = parted if two is not None and q == two[0] and b == two[1] else side[q]
            wv[q][:, :, on[b]] = np.abs(wv[q][:, :, on[b]]) * sign[:, None, None, :] * (1 - 2 * (int(then[q]) >> b & 1))
    return {**d, "wv": big(wv.reshape(N, 128, 2048), 1), "p2": np.stack([p2.reshape(128, 512).astype(BF)] * N)}
def setup_inputs(rng):
    return plain(rng)
def setup_inputs_crowd(rng):
    h, g = (int(v) for v in rng.permutation(N)[:2])
    c, then = rng.permutation(N), np.zeros(N, np.int64)
    then[c] = np.roll(c, 1)
    bit = int(rng.choice([b for b in range(L) if int(then[h]) ^ (1 << b) != h]))
    one = int(rng.choice([q for q in range(N) if q not in (h, g) and int(then[q]) != int(then[h]) ^ (1 << bit)]))
    others = np.delete(np.arange(N), [h, g, one])
    o, n = rng.permutation(N), np.full(N, CAPP)
    n[o[N // 2:]] += rng.integers(1, P - CAPP + 1, N - N // 2)
    n[o[-1]] = P
    r, more = int(o[N // 2]), P // (CAPP + 1) - 1
    if more: n[r] = rng.integers(CAPP + 1, P - more * (CAPP + 1) + 1)
    want = rng.choice(others, (N, P))
    for s in range(N): want[s, rng.permutation(P)[:n[s]]] = h
    e = rng.permutation(np.flatnonzero((want != h) & (np.arange(N) != r)[:, None]))
    want.flat[e[:CB]] = g
    want.flat[e[CB]] = one
    if more:
        e = rng.permutation(np.flatnonzero(want[r] != h))
        want[r, e[:more * (CAPP + 1)]] = np.repeat(rng.choice(others, more, replace=False), CAPP + 1)
    kind = np.zeros((N, P), np.int64)
    for s in range(N):
        e = np.flatnonzero(want[s] == h)
        kind[s, e] = 1 - 2 * ((np.arange(e.size) + int(rng.integers(0, 2))) % 2)
    return aimed(rng, plain(rng), want, then=then, two=(h, bit, kind))
def setup_inputs_few(rng):
    o = rng.permutation(N)
    want = rng.choice(o[2:], (N, P))
    want[int(rng.integers(0, N)), int(rng.integers(0, P))] = o[0]
    return aimed(rng, plain(rng), want)
def setup_inputs_neg(rng):
    d, g = plain(rng), rng.permutation(16)
    want = np.stack([rng.permutation(P) % N for s in range(N)])
    part = 8 * g[:, None] + np.arange(8)
    rows = (4 * part[L:].reshape(-1)[:, None] + np.arange(4)).reshape(-1)
    x, p = np.zeros((N, P, 512)), np.zeros((128, 128, 4))
    for b in range(L):
        v = rng.choice([-1.0, 1.0], (8, 4))
        p[part[b], b] = v * (1 + rng.random((8, 4)))
        e = (4 * part[b][:, None] + np.arange(4)).reshape(-1)
        x[:, :, e] = 2.0 ** -8 * v.reshape(-1) * (1 - 2 * (want >> b & 1))[:, :, None]
    for q in range(N):
        s, i = np.nonzero(want == q)
        v = np.full((P, P), -2.0 ** -7)
        v[np.arange(P), np.arange(P)] = P * 2.0 ** -7
        x[s[:, None], i[:, None], rng.permutation(rows)[:P][None, :]] = v * rng.choice([-1.0, 1.0], P)
    x *= np.exp2(rng.integers(-1, 2, (N, P, 1)))
    x = np.ascontiguousarray(x.reshape(N, P, 128, 4).transpose(0, 2, 1, 3)).reshape(N, 128, 4 * P)
    return {**d, "x": x.astype(np.float32).astype(BF), "pl": np.stack([p.reshape(128, 512).astype(np.float32).astype(BF)] * N)}
def setup_inputs_zero(rng):
    gone = np.zeros((N, P), np.int64)
    for s in range(N):
        e = rng.permutation(P)
        gone[s, e[:P // 4]] = N - 1
        gone[s, e[P // 4:P // 2]] = 1 << rng.integers(0, L, P // 2 - P // 4)
    d = aimed(rng, plain(rng), rng.integers(0, N, (N, P)), gone)
    b, q, on = int(rng.integers(0, L)), int(rng.integers(0, N)), rng.permutation(128)[:16]
    p2, wv = np.array(d["p2"]).reshape(N, 128, 128, 4), np.array(d["wv"]).reshape(N, 128, 4, 128, 4)
    p2[:, np.setdiff1d(np.arange(128), on), b] = 0
    wv[q][:, :, on] = 0
    return {**d, "p2": p2.reshape(N, 128, 512), "wv": wv.reshape(N, 128, 2048)}
def setup_inputs_spread(rng):
    return {**plain(rng), "x": big(wide(rng, N, 128, 4 * P, cols=2), 2.0 ** -10)}
def check_inputs(d):
    b = []
    for k in ("x", "pl", "p2", "wv", "w"):
        v = np.abs(d[k].astype(np.float32))
        if not (np.isfinite(v).all() and ((v == 0) | (v >= 2.0 ** -30) & (v <= 2.0 ** 30)).all()): b.append("a value of " + k)
    for k in ("pl", "p2"):
        p = d[k].astype(np.float32)
        if (p[:, :, 4 * L:] != 0).any(): b.append(k + " has numbers behind its first L columns")
        if (p != p[:1]).any(): b.append(k + " isn't the same on all ranks")
    return b
def reference(x, pl, p2, wv, w):
    X, bk = buckets(x, pl)
    at = taken(bk)
    H, num, to = [], [], []
    for d in range(N):
        c = join(*[pick(X[s], at[d, s]) for s in range(N)])
        A, V, h = attend(c, wv[d], np.flatnonzero(at[d].reshape(-1) >= 0))
        h = mx_ref.quantize(h)
        n = np.concatenate([np.where(at[d, s] >= 0, P * s + at[d, s], -1) for s in range(N)])
        H.append(h)
        num.append(n)
        to.append(np.where(n >= 0, number(mx_ref.matmul(mx_ref.quantize(np.ascontiguousarray(p2[d])), h)), -1))
    H = join(*H)
    num = np.concatenate(num + [np.full(1, -1)])
    oc, osc = np.zeros((N, 128, 4 * N * CB), np.uint8), np.zeros((N, 16, N * CB), np.uint8)
    nb, y = np.zeros((N, 1, N * CB), np.float32), np.zeros((N, 128, N * CB), np.float32)
    for e in range(N):
        k = np.full(N * CB, -1)
        for d in range(N):
            i = np.flatnonzero(to[d] == e)[:CB]
            k[d * CB + np.arange(i.size)] = 512 * d + i
        h = pick(H, k)
        oc[e], osc[e] = emit(h)
        nb[e, 0] = num[k]
        y[e] = mx_ref.matmul(mx_ref.quantize(np.ascontiguousarray(w[e])), h)
    return {"oc": oc, "osc": osc, "id": nb, "y": y}

@@ -1,0 +1,348 @@
+from concourse.bass import DstId, RemoteDMATransfer
+from concourse.mybir import dt, AluOpType, ActivationFunctionType
+
+BF, F4, I4, U2, CO, PL = "bfloat16", "float32", "int32", "uint16", "float8_e4m3fn_x4", "uint8"
+SCRATCH = {
+    "zr": ("sbuf", [128, 256], BF), "rp": ("sbuf", [128, 2048], BF),
+    "xt": ("sbuf", [128, 1032], BF), "xq": ("sbuf", [128, 258], CO), "xs": ("sbuf", [128, 258], PL),
+    "plin": ("sbuf", [128, 16], BF), "plt": ("sbuf", [128, 1536], BF), "plq": ("sbuf", [128, 384], CO), "pls": ("sbuf", [128, 384], PL),
+    "p2in": ("sbuf", [128, 16], BF), "p2t": ("sbuf", [128, 1536], BF), "p2q": ("sbuf", [128, 384], CO), "p2s": ("sbuf", [128, 384], PL),
+    "wvt": ("sbuf", [128, 2048], BF), "wvq": ("sbuf", [128, 512], CO), "wvs": ("sbuf", [128, 512], PL),
+    "wt": ("sbuf", [128, 512], BF), "wq": ("sbuf", [128, 128], CO), "ws": ("sbuf", [128, 128], PL),
+    "send1": ("sbuf", [128, 512], CO), "send1s": ("sbuf", [128, 512], PL),
+    "land1": ("sbuf", [128, 512], CO), "land1s": ("sbuf", [128, 512], PL),
+    "ctq": ("sbuf", [128, 512], CO), "cts": ("sbuf", [128, 512], PL),
+    "vt": ("sbuf", [128, 2048], BF), "vq": ("sbuf", [128, 512], CO), "vs": ("sbuf", [128, 512], PL),
+    "at": ("sbuf", [128, 2048], BF), "aq": ("sbuf", [128, 512], CO), "asc": ("sbuf", [128, 512], PL),
+    "ht": ("sbuf", [128, 2056], BF), "hq": ("sbuf", [128, 514], CO), "hs": ("sbuf", [128, 514], PL),
+    "send2": ("sbuf", [128, 512], CO), "send2s": ("sbuf", [128, 512], PL),
+    "land2": ("sbuf", [128, 512], CO), "land2s": ("sbuf", [128, 512], PL),
+    "yt": ("sbuf", [128, 512], F4),
+    "ii": ("sbuf", [128, 8], I4), "ict": ("sbuf", [128, 32], I4), "ib": ("sbuf", [128, 32], I4),
+    "i16": ("sbuf", [128, 16], F4), "cb": ("sbuf", [128, 32], F4),
+    "cf": ("sbuf", [128, 8], F4), "thr": ("sbuf", [128, 16], BF), "thb": ("sbuf", [128, 16], F4), "dcol": ("sbuf", [128, 2], BF),
+    "fct": ("sbuf", [128, 32], F4), "fb": ("sbuf", [128, 32], F4), "offct": ("sbuf", [128, 32], U2), "offb": ("sbuf", [128, 32], U2),
+    "ll1": ("sbuf", [128, 32], F4), "lt1": ("sbuf", [128, 32], F4), "off1": ("sbuf", [128, 32], U2),
+    "ll2": ("sbuf", [128, 32], F4), "lt2": ("sbuf", [128, 32], F4), "off2": ("sbuf", [128, 32], U2), "asum": ("sbuf", [128, 8], F4),
+    "llr": ("sbuf", [128, 32], F4), "tr": ("sbuf", [128, 32], F4), "tv": ("sbuf", [128, 32], F4), "ta": ("sbuf", [128, 32], F4),
+    "id1": ("sbuf", [128, 32], F4), "idg": ("sbuf", [128, 512], F4), "idrow": ("sbuf", [128, 520], F4), "inv0": ("sbuf", [128, 512], BF),
+    "idsel": ("sbuf", [128, 512], F4), "idin": ("sbuf", [8, 128], F4), "idout": ("sbuf", [8, 64], F4),
+    "lst1": ("dram", [8, 128, 1], F4), "ldl1": ("dram", [8, 128, 1], F4), "lst2": ("dram", [4, 128, 1], F4), "ldl2": ("dram", [8, 128, 1], F4),
+}
+for _h in range(3):
+    SCRATCH["u%d" % _h] = ("sbuf", [128, 768], BF)
+    SCRATCH["k%d" % _h] = ("sbuf", [128, 1024], BF)
+    SCRATCH["z%d" % _h] = ("sbuf", [128, 2048], BF)
+    SCRATCH["zs%d" % _h] = ("sbuf", [128, 2048], BF)
+    SCRATCH["jk%d" % _h] = ("sbuf", [128, 2048], BF)
+    SCRATCH["acc%d" % _h] = ("sbuf", [128, 8], F4)
+for _h in range(8):
+    SCRATCH["ps%d" % _h] = ("psum", [128, 512], F4)
+SEMAPHORES = ["v", "s", "t", "gi", "dx", "dpl", "dwv", "dw", "dp2", "dl1", "dl1o", "dlr", "dl2", "dl2o", "dli", "did",
+              "doc", "dy", "snd", "a1", "l1", "a2on", "a2off", "l2"]
+
+
+def rank_program(g, core, T, topo):
+    r = T.rank_of(core)
+    if r is None:
+        return
+    cores = T.cores
+    n_ranks = len(cores)
+    Q = {"v": g.vector, "s": g.scalar, "t": g.tensor, "y": g.sync, "g": g}
+    V, S, PE = g.vector, g.scalar, g.tensor
+    op, fn = AluOpType, ActivationFunctionType
+    waited, count = {}, {}
+
+    def need(q, deps):
+        best = {}
+        for d in deps:
+            if d is not None:
+                best[d[0]] = max(best.get(d[0], 0), d[1])
+        for s in best:
+            if waited.get((q, s), 0) < best[s]:
+                Q[q].wait_ge(T.sem[s], best[s])
+                waited[(q, s)] = best[s]
+
+    def raised(ins, s, n):
+        ins.then_inc(T.sem[s], n)
+        count[s] = count.get(s, 0) + n
+        return (s, count[s])
+
+    def v(deps, f, *a):
+        need("v", deps)
+        return raised(f(*a), "v", 1)
+
+    def s(deps, out, in_, func, **k):
+        need("s", deps)
+        return raised(S.activation(out, in_, func, **k), "s", 1)
+
+    def mm(deps, out, a, asc, b, bsc):
+        need("t", deps)
+        return raised(PE.matmul_mx(out, a, asc, b, bsc, True, True), "t", 1)
+
+    def dma(q, deps, sem, out, in_):
+        need(q, deps)
+        return raised(Q[q].dma_start(out, in_), sem, 16)
+
+    def io(pat, out, base=0, ch=0, f32=False):
+        if f32:
+            return raised(g.iota(out, pat, base, ch, allow_small_or_imprecise_dtypes=True), "gi", 1)
+        return raised(g.iota(out, pat, base, ch), "gi", 1)
+
+    near = [q for q in range(n_ranks) if topo.chip(cores[q]) == topo.chip(core)]
+    far = [q for q in range(n_ranks) if q not in near]
+    near_to = [q for q in near if q != r]
+    n0, f0 = min(near), min(far)
+    far_pool = topo.engines(core, cores[far[0]])
+    near_pool = [e for e in topo.engines(core, cores[near_to[0]]) if e not in far_pool]
+
+    def share(pool, k):
+        w = 1
+        while 2 * w * k <= len(pool):
+            w *= 2
+        return w
+
+    wf, wn = share(far_pool, len(far)), share(near_pool, len(near_to))
+
+    def send(dests, src, dst, sem_of, codes):
+        tr, tot = [], 0
+        used = {"f": 0, "n": 0}
+        for q in dests:
+            k, pool, w = ("f", far_pool, wf) if q in far else ("n", near_pool, wn)
+            mask = 0
+            for e in pool[used[k]:used[k] + w]:
+                mask += 1 << e
+            used[k] += w
+            tot += w
+            rid, pid, _ = topo.addr(cores[q])
+            a, b = src[:, 64 * q:64 * q + 64], dst[:, 64 * r:64 * r + 64]
+            if codes:
+                a, b = a.bitcast(dt.uint8), b.bitcast(dt.uint8)
+            tr.append(RemoteDMATransfer(dst_ids=[DstId(rid=rid, pnc=pid)], dma_engine_mask=mask, remote_sem=T.sem[sem_of(q)], src=a, dst=b))
+        g.remote_dma_fused(tr, local_sem=T.sem.snd)
+        count["snd"] = count.get("snd", 0) + tot
+
+    def send_lists(src_of, dst, sem):
+        tr = []
+        used = {"f": 0, "n": 0}
+        for q in far + near_to:
+            k, pool = ("f", far_pool) if q in far else ("n", near_pool)
+            mask = 1 << pool[used[k]]
+            used[k] += 1
+            rid, pid, _ = topo.addr(cores[q])
+            tr.append(RemoteDMATransfer(dst_ids=[DstId(rid=rid, pnc=pid)], dma_engine_mask=mask, remote_sem=T.sem[sem], src=src_of(q), dst=dst[r]))
+        g.remote_dma_fused(tr, local_sem=T.sem.snd)
+        count["snd"] = count.get("snd", 0) + len(tr)
+
+    dpl = dma("s", [], "dpl", T.plin[:, 0:12], T.pl[:, 0:12])
+    dx = dma("y", [], "dx", T.xt[:, 0:1024], T.x[:])
+    dwv = dma("y", [dx], "dwv", T.wvt[:], T.wv[:])
+    dw = dma("y", [], "dw", T.wt[:], T.w[:])
+    dp2 = dma("y", [], "dp2", T.p2in[:, 0:12], T.p2[:, 0:12])
+
+    i0 = io([[1, 1]], T.ii[:, 0:1], 0, 1)
+    i1 = io([[1, 16]], T.i16[:], f32=True)
+    i2 = io([[1, 4], [64, 8]], T.ict[:])
+    i3 = io([[2, 16], [0, 2]], T.ib[:])
+    i4 = io([[256, 8], [0, 4]], T.cb[:], base=1, f32=True)
+    zr = v([], V.memset, T.zr[:], 0.0)
+    xz = v([], V.memset, T.xt[:, 1024:1032], 0.0)
+    c1 = v([i0], V.tensor_scalar, T.ii[:, 1:2], T.ii[:, 0:1], 31, 2, op.bitwise_and, op.arith_shift_right)
+    c2 = v([], V.tensor_scalar, T.ii[:, 2:3], T.ii[:, 0:1], 3, None, op.bitwise_and)
+    c3 = v([], V.tensor_scalar, T.ii[:, 3:4], T.ii[:, 0:1], 4, 1, op.arith_shift_right, op.bitwise_and)
+    c4 = v([], V.tensor_scalar, T.ii[:, 4:5], T.ii[:, 0:1], 15, None, op.bitwise_and)
+    dcol = v([c1], V.tensor_scalar, T.dcol[:, 0:1], T.ii[:, 1:2], 8.0, None, op.subtract)
+    m0 = v([c1], V.tensor_scalar, T.cf[:, 2:3], T.ii[:, 1:2], 0.0, None, op.is_equal)
+    f1 = v([c2], V.tensor_scalar, T.cf[:, 1:2], T.ii[:, 2:3], 16.0, None, op.mult)
+    f3 = v([c3], V.tensor_copy, T.cf[:, 3:4], T.ii[:, 3:4])
+    f4 = v([c4], V.tensor_scalar, T.cf[:, 4:5], T.ii[:, 4:5], 4.0, None, op.mult)
+    thr = v([i1, f1], V.tensor_scalar, T.thr[:], T.i16[:], T.cf[:, 1:2], None, op.add)
+    thb = v([i1, f1], V.tensor_scalar, T.thb[:], T.i16[:], T.cf[:, 1:2], 0.5, op.add, op.add)
+    r1 = v([], V.memset, T.rp[:], 1.0)
+    rp = v([r1], V.memset, T.rp[:, 0:2048:256], 0.0)
+
+    def planes(din, src, tile, cod, sca):
+        toks = []
+        for b in range(3):
+            for t in range(4):
+                k = 4 * b + t
+                o = tile[:, 512 * b + t:512 * b + 512:4]
+                if t < 3:
+                    toks.append(v([din, zr], V.tensor_scalar, o, T.zr[:, 0:128], src[:, k:k + 1], None, op.add))
+                else:
+                    toks.append(s([din, zr], o, T.zr[:, 0:128], fn.Identity, bias=src[:, k:k + 1]))
+        return v(toks, V.quantize_mx, cod[:], sca[:], tile[:])
+
+    plq = planes(dpl, T.plin, T.plt, T.plq, T.pls)
+    xq = v([dx, xz], V.quantize_mx, T.xq[:], T.xs[:], T.xt[:])
+
+    def running(h, zt, zp, init, inv, deps):
+        u, k = T["u%d" % h], T["k%d" % h]
+        a = v([zt[0]], V.tensor_scalar, u[:, 0:256], zp[0][:, 0:256], 0.0, -8.0, op.is_lt, op.add)
+        b = v([zt[1]], V.tensor_scalar, u[:, 256:512], zp[1][:, 0:256], 0.0, 2.0, op.is_lt, op.mult)
+        c = v([zt[2]], V.tensor_scalar, u[:, 512:768], zp[2][:, 0:256], 0.0, 4.0, op.is_lt, op.mult)
+        d = v([a, b], V.tensor_tensor_scan, k[:, 0:256], u[:, 256:512], u[:, 0:256], -100.0, op.max, op.add)
+        e = v([c, d], V.tensor_tensor_scan, k[:, 256:512], u[:, 512:768], k[:, 0:256], -100.0, op.max, op.add)
+        f = v([e, dcol], V.tensor_scalar, k[:, 512:768], k[:, 256:512], T.dcol[:, 0:1], None, op.is_equal)
+        return v([f, zr] + deps, V.tensor_tensor_scan, k[:, 768:1024], k[:, 512:768], inv, init, op.add, op.subtract)
+
+    def counts(h, ct):
+        cc = T["k%d" % h][:, 768:1024]
+        z, zs, jk, acc = T["z%d" % h], T["zs%d" % h], T["jk%d" % h], T["acc%d" % h]
+        st = None
+        for a in range(8):
+            st = s([ct, thb], jk[:, 256 * a:256 * a + 256], cc, fn.Sign, bias=T.thb[:, 8 + a:9 + a], scale=-1.0, accum_out=acc[:, a:a + 1])
+        vt_ = None
+        for a in range(8):
+            vt_ = v([ct, thr], V.tensor_scalar, z[:, 256 * a:256 * a + 256], cc, T.thr[:, a:a + 1], None, op.is_le)
+        return v([vt_, rp], V.tensor_tensor_scan, zs[:], T.rp[:], z[:], 0.0, op.mult, op.add), st
+
+    def offsets(ll, lt, off, deps):
+        a = v(deps, V.transpose, lt[:], ll[:])
+        return v([a], V.tensor_copy, off[:], lt[:])
+
+    zt = [mm([plq, xq], T["ps%d" % b][:, 0:256], T.plq[:, 128 * b:128 * b + 128], T.pls[:, 128 * b:128 * b + 128], T.xq[:, 0:256], T.xs[:, 0:256]) for b in range(3)]
+    ct = running(0, zt, [T.ps0, T.ps1, T.ps2], 0.0, T.zr[:, 0:256], [])
+    cv, cs = counts(0, ct)
+    l1 = s([cs], T.ll1[:, 8:16], T.acc0[:], fn.Identity, scale=0.5, bias=128.0)
+    l2 = s([cs], T.ll1[:, 24:32], T.acc0[:], fn.Identity, scale=0.5, bias=128.0)
+    l3 = v([cv], V.tensor_copy, T.ll1[:, 0:8], T.zs0[:, 255:2048:256])
+    l4 = v([cv], V.tensor_copy, T.ll1[:, 16:24], T.zs0[:, 255:2048:256])
+    o1 = offsets(T.ll1, T.lt1, T.off1, [l1, l2, l3, l4])
+    dl1 = dma("y", [l1, l2, l3, l4], "dl1", T.lst1[:], T.ll1[0:32, 0:32])
+    dl1o = dma("y", [dl1], "dl1o", T.ldl1[r], T.lst1[r])
+
+    def pick(ot, deps, dq, ds, c0, wq_, ws_, wn_, off, e0, n):
+        e1 = e0 + n // 16
+        a = v([ot] + deps, V.tensor_copy, dq[:, c0:c0 + n].bitcast(dt.uint32), wq_[:, 0:wn_].bitcast(dt.uint32).indirect(off[:, e0:e1]))
+        b = s([ot] + deps, ds[:, c0:c0 + n], ws_[:, 0:wn_].indirect(off[:, e0:e1]), fn.Copy)
+        return a, b
+
+    def dispatch(ot, deps, sq, ss, lq, ls, wq_, ws_, wn_, off, sem_of):
+        pf = pick(ot, deps, sq, ss, 64 * f0, wq_, ws_, wn_, off, 4 * f0, 64 * len(far))
+        need("g", [pf[0]])
+        send(far, sq, lq, sem_of, True)
+        need("g", [pf[1]])
+        send(far, ss, ls, sem_of, False)
+        pn = pick(ot, deps, sq, ss, 64 * n0, wq_, ws_, wn_, off, 4 * n0, 64 * len(near))
+        need("g", [pn[0]])
+        send(near_to, sq, lq, sem_of, True)
+        need("g", [pn[1]])
+        send(near_to, ss, ls, sem_of, False)
+        return pick(ot, deps, lq, ls, 64 * r, wq_, ws_, wn_, off, 4 * r, 64)
+
+    own1 = dispatch(o1, [xq], T.send1, T.send1s, T.land1, T.land1s, T.xq, T.xs, 258, T.off1, lambda q: "a1")
+    need("g", [dl1])
+    send_lists(lambda q: T.lst1[q], T.ldl1, "l1")
+    arr1 = ("a1", 2 * (wf * len(far) + wn * len(near_to)))
+    lst1 = ("l1", n_ranks - 1)
+    count["a1"], count["l1"] = arr1[1], lst1[1]
+
+    g1 = v([i2, f4], V.tensor_scalar, T.fct[:], T.ict[:], T.cf[:, 4:5], None, op.add)
+    g2 = v([i3, f3], V.tensor_scalar, T.fb[:], T.ib[:], T.cf[:, 3:4], None, op.add)
+    oct_ = v([g1], V.tensor_copy, T.offct[:], T.fct[:])
+    ob = v([g2], V.tensor_copy, T.offb[:], T.fb[:])
+    hz = v([], V.memset, T.ht[:, 2048:2056], 0.0)
+    iz = v([], V.memset, T.idrow[:, 512:520], 0.0)
+    wvq = v([dwv], V.quantize_mx, T.wvq[:], T.wvs[:], T.wvt[:])
+    wq = v([dw], V.quantize_mx, T.wq[:], T.ws[:], T.wt[:])
+    p2q = planes(dp2, T.p2in, T.p2t, T.p2q, T.p2s)
+
+    dlr = None
+    for a in range(4):
+        dlr = dma("y", [lst1, dl1o], "dlr", T.llr[32 * a:32 * a + 32, 0:32], T.ldl1[:])
+
+    cpk = []
+    for t in range(4):
+        a = v([arr1, oct_, own1[0]], V.tensor_copy, T.ctq[:, 128 * t:128 * t + 128].bitcast(dt.uint32), T.land1[:].bitcast(dt.uint32).indirect(T.offct[:, 8 * t:8 * t + 8]))
+        b = s([arr1, oct_, own1[1]], T.cts[:, 128 * t:128 * t + 128], T.land1s[:].indirect(T.offct[:, 8 * t:8 * t + 8]), fn.Copy)
+        cpk.append([a, b])
+
+    def c_t(t):
+        return T.ctq[:, 128 * t:128 * t + 128], T.cts[:, 128 * t:128 * t + 128]
+
+    P = [T["ps%d" % b] for b in range(8)]
+    sm = [mm(cpk[t] + [wvq, arr1], P[t][:], c_t(t)[0], c_t(t)[1], T.wvq[:], T.wvs[:]) for t in range(4)]
+    se = [None] * 4
+    for t in range(4):
+        o = T.vt[:, t:2048:4]
+        se[t] = s([sm[t]], o, P[t][:], fn.Copy) if t % 2 == 0 else v([sm[t]], V.tensor_copy, o, P[t][:])
+    vq = v(se, V.quantize_mx, T.vq[:], T.vs[:], T.vt[:])
+    aq = []
+    for h in range(2):
+        rm, re = [], []
+        for t in range(4):
+            b = P[(4 if h == 0 else 0) + t]
+            rm.append(mm([own1[0], own1[1], arr1, se[t] if h else None], b[:, 0:256], c_t(t)[0], c_t(t)[1], T.land1[:, 256 * h:256 * h + 256], T.land1s[:, 256 * h:256 * h + 256]))
+        for t in range(4):
+            b = P[(4 if h == 0 else 0) + t]
+            o = T.at[:, 1024 * h + t:1024 * h + 1024:4]
+            if t < 3:
+                re.append(s([rm[t]], o, b[:, 0:256], fn.Relu, scale=0.0625))
+            else:
+                re.append(v([rm[t]], V.tensor_scalar, o, b[:, 0:256], 0.0, 0.0625, op.max, op.mult))
+        aq.append((v(re, V.quantize_mx, T.aq[:, 256 * h:256 * h + 256], T.asc[:, 256 * h:256 * h + 256], T.at[:, 1024 * h:1024 * h + 1024]), re))
+
+    a = v([dlr], V.transpose, T.tr[:], T.llr[:])
+    b = v([a], V.tensor_scalar, T.tv[:], T.tr[:], 255.5, None, op.is_lt)
+    c = v([a, i4], V.tensor_tensor, T.ta[:], T.tr[:], T.cb[:], op.add)
+    d = v([b, c], V.tensor_tensor, T.id1[:], T.tv[:], T.ta[:], op.mult)
+    e = v([d, ob], V.tensor_copy, T.idg[:], T.id1[:].indirect(T.offb[:]))
+    idr = v([e], V.transpose, T.idrow[:, 0:512], T.idg[:])
+    inv = v([idr, m0], V.tensor_scalar, T.inv0[:], T.idrow[:, 0:512], 0.5, T.cf[:, 2:3], op.is_lt, op.mult)
+
+    he, hq = [], []
+    om = []
+    for h in range(2):
+        om.append([mm([vq, aq[h][0]] + aq[h][1], P[(4 if h == 0 else 0) + i][:, 0:256], T.vq[:, 128 * i:128 * i + 128], T.vs[:, 128 * i:128 * i + 128],
+                      T.aq[:, 256 * h:256 * h + 256], T.asc[:, 256 * h:256 * h + 256]) for i in range(4)])
+    zt2 = []
+    for h in range(2):
+        ev = []
+        for i in range(4):
+            b = P[(4 if h == 0 else 0) + i]
+            o = T.ht[:, 1024 * h + i:1024 * h + 1024:4]
+            if h == 0 or i % 2 == 0:
+                ev.append(s([om[h][i]], o, b[:, 0:256], fn.Identity, scale=0.0625))
+            else:
+                ev.append(v([om[h][i]], V.tensor_scalar, o, b[:, 0:256], 0.0625, None, op.mult))
+        he.append(ev)
+        hi = 256 if h == 0 else 514
+        hq.append(v(ev + [hz], V.quantize_mx, T.hq[:, 256 * h:hi], T.hs[:, 256 * h:hi], T.ht[:, 1024 * h:4 * hi]))
+        zt2.append([mm([p2q, hq[h]], P[(4 if h == 0 else 0) + b][:, 0:256], T.p2q[:, 128 * b:128 * b + 128], T.p2s[:, 128 * b:128 * b + 128],
+                       T.hq[:, 256 * h:256 * h + 256], T.hs[:, 256 * h:256 * h + 256]) for b in range(3)])
+    ct1 = running(1, zt2[0], P[4:7], 0.0, T.inv0[:, 0:256], [inv])
+    ct2 = running(2, zt2[1], P[0:3], T.k1[:, 1023:1024], T.inv0[:, 256:512], [inv, ct1])
+    cv1, cs1 = counts(1, ct1)
+    cv2, cs2 = counts(2, ct2)
+    l3 = v([cv1, cv2], V.tensor_tensor, T.ll2[:, 0:8], T.zs1[:, 255:2048:256], T.zs2[:, 255:2048:256], op.add)
+    l4 = v([cv1, cv2], V.tensor_tensor, T.ll2[:, 16:24], T.zs1[:, 255:2048:256], T.zs2[:, 255:2048:256], op.add)
+    sa = v([cs1, cs2], V.tensor_tensor, T.asum[:], T.acc1[:], T.acc2[:], op.add)
+    l1 = v([sa], V.tensor_scalar, T.ll2[:, 8:16], T.asum[:], 0.5, 256.0, op.mult, op.add)
+    l2 = v([sa], V.tensor_scalar, T.ll2[:, 24:32], T.asum[:], 0.5, 256.0, op.mult, op.add)
+    o2 = offsets(T.ll2, T.lt2, T.off2, [l1, l2, l3, l4])
+
+    own2 = dispatch(o2, [hq[1]], T.send2, T.send2s, T.land2, T.land2s, T.hq, T.hs, 514, T.off2, lambda q: "a2off" if q in far else "a2on")
+    ids = s([o2, idr, iz], T.idsel[:], T.idrow[:].indirect(T.off2[:]), fn.Copy)
+    dl2 = dma("y", [ids], "dl2", T.lst2[:], T.idsel[0:1, 0:512])
+    dl2o = dma("y", [dl2], "dl2o", T.ldl2[r], T.lst2[r // 2])
+    need("g", [dl2])
+    send_lists(lambda q: T.lst2[q // 2], T.ldl2, "l2")
+    an = ("a2on", 2 * wn * len(near_to))
+    af = ("a2off", 2 * wf * len(far))
+    lst2 = ("l2", n_ranks - 1)
+    count["a2on"], count["a2off"], count["l2"] = an[1], af[1], lst2[1]
+
+    for k, (c0, w, deps) in enumerate(((64 * n0, 64 * len(near), [an, own2[0], own2[1]]), (64 * f0, 64 * len(far), [af]))):
+        b = P[7 - 4 * k]
+        ym = mm([wq, he[k][3]] + deps, b[:, 0:w], T.wq[:], T.ws[:], T.land2[:, c0:c0 + w], T.land2s[:, c0:c0 + w])
+        ye = v([ym], V.tensor_copy, T.yt[:, c0:c0 + w], b[:, 0:w])
+        dma("s", deps, "doc", T.oc[:, 4 * c0:4 * c0 + 4 * w], T.land2[:, c0:c0 + w].bitcast(dt.uint8))
+        if k:
+            for m in range(4):
+                dma("s", deps, "doc", T.osc[4 * m:4 * m + 4, :], T.land2s[32 * m:32 * m + 4, :])
+        dma("s", [ye], "dy", T.y[:, c0:c0 + w], T.yt[:, c0:c0 + w])
+    dli = dma("y", [lst2, dl2o], "dli", T.idin[:], T.ldl2[:])
+    ido = v([dli], V.tensor_scalar, T.idout[:], T.idin[:, 64 * (r % 2):64 * (r % 2) + 64], -1.0, None, op.add)
+    dma("y", [ido], "did", T.id[:], T.idout[:])
+    need("y", [(k, count[k]) for k in count])

@@ -1,44 +1,32 @@
 from concourse.bass import DstId, RemoteDMATransfer
 from concourse.mybir import dt, AluOpType, ActivationFunctionType
 
+NV = [8, 6, 7]
+
 BF, F4, I4, U2, CO, PL = "bfloat16", "float32", "int32", "uint16", "float8_e4m3fn_x4", "uint8"
-SCRATCH = {
-    "zr": ("sbuf", [128, 256], BF), "rp": ("sbuf", [128, 2048], BF),
-    "xt": ("sbuf", [128, 1032], BF), "xq": ("sbuf", [128, 258], CO), "xs": ("sbuf", [128, 258], PL),
-    "plin": ("sbuf", [128, 16], BF), "plt": ("sbuf", [128, 1536], BF), "plq": ("sbuf", [128, 384], CO), "pls": ("sbuf", [128, 384], PL),
-    "p2in": ("sbuf", [128, 16], BF), "p2t": ("sbuf", [128, 1536], BF), "p2q": ("sbuf", [128, 384], CO), "p2s": ("sbuf", [128, 384], PL),
-    "wvt": ("sbuf", [128, 2048], BF), "wvq": ("sbuf", [128, 512], CO), "wvs": ("sbuf", [128, 512], PL),
-    "wt": ("sbuf", [128, 512], BF), "wq": ("sbuf", [128, 128], CO), "ws": ("sbuf", [128, 128], PL),
-    "send1": ("sbuf", [128, 512], CO), "send1s": ("sbuf", [128, 512], PL),
-    "land1": ("sbuf", [128, 512], CO), "land1s": ("sbuf", [128, 512], PL),
-    "ctq": ("sbuf", [128, 512], CO), "cts": ("sbuf", [128, 512], PL),
-    "vt": ("sbuf", [128, 2048], BF), "vq": ("sbuf", [128, 512], CO), "vs": ("sbuf", [128, 512], PL),
-    "at": ("sbuf", [128, 2048], BF), "aq": ("sbuf", [128, 512], CO), "asc": ("sbuf", [128, 512], PL),
-    "ht": ("sbuf", [128, 2056], BF), "hq": ("sbuf", [128, 514], CO), "hs": ("sbuf", [128, 514], PL),
-    "send2": ("sbuf", [128, 512], CO), "send2s": ("sbuf", [128, 512], PL),
-    "land2": ("sbuf", [128, 512], CO), "land2s": ("sbuf", [128, 512], PL),
-    "yt": ("sbuf", [128, 512], F4),
-    "ii": ("sbuf", [128, 8], I4), "ict": ("sbuf", [128, 32], I4), "ib": ("sbuf", [128, 32], I4),
-    "i16": ("sbuf", [128, 16], F4), "cb": ("sbuf", [128, 32], F4),
-    "cf": ("sbuf", [128, 8], F4), "thr": ("sbuf", [128, 16], BF), "thb": ("sbuf", [128, 16], F4), "dcol": ("sbuf", [128, 2], BF),
-    "fct": ("sbuf", [128, 32], F4), "fb": ("sbuf", [128, 32], F4), "offct": ("sbuf", [128, 32], U2), "offb": ("sbuf", [128, 32], U2),
-    "ll1": ("sbuf", [128, 32], F4), "lt1": ("sbuf", [128, 32], F4), "off1": ("sbuf", [128, 32], U2),
-    "ll2": ("sbuf", [128, 32], F4), "lt2": ("sbuf", [128, 32], F4), "off2": ("sbuf", [128, 32], U2), "asum": ("sbuf", [128, 8], F4),
-    "llr": ("sbuf", [128, 32], F4), "tr": ("sbuf", [128, 32], F4), "tv": ("sbuf", [128, 32], F4), "ta": ("sbuf", [128, 32], F4),
-    "id1": ("sbuf", [128, 32], F4), "idg": ("sbuf", [128, 512], F4), "idrow": ("sbuf", [128, 520], F4), "inv0": ("sbuf", [128, 512], BF),
-    "idsel": ("sbuf", [128, 512], F4), "idin": ("sbuf", [8, 128], F4), "idout": ("sbuf", [8, 64], F4),
-    "lst1": ("dram", [8, 128, 1], F4), "ldl1": ("dram", [8, 128, 1], F4), "lst2": ("dram", [4, 128, 1], F4), "ldl2": ("dram", [8, 128, 1], F4),
-}
+SCRATCH = {}
+for _n, _w, _d in (("zr", 256, BF), ("rp", 2048, BF), ("xt", 1032, BF), ("plin", 16, BF), ("plt", 1536, BF), ("p2in", 16, BF),
+                   ("p2t", 1536, BF), ("wvt", 2048, BF), ("wt", 512, BF), ("vt", 2048, BF), ("at", 2048, BF), ("ht", 2056, BF),
+                   ("yt", 512, F4), ("ii", 8, I4), ("ict", 32, I4), ("ib", 32, I4), ("i16", 16, F4), ("ev", 32, F4), ("cf", 8, F4),
+                   ("thr", 16, BF), ("thb", 16, F4), ("dcol", 2, BF), ("fct", 32, F4), ("fb", 32, F4), ("fe", 32, F4), ("fm", 32, F4),
+                   ("fo", 32, F4), ("fg", 2, F4), ("offct", 32, U2), ("offi", 32, U2), ("offg", 2, U2), ("ll1", 32, F4), ("lt1", 32, F4),
+                   ("off1", 32, U2), ("ll2", 32, F4), ("lt2", 32, F4), ("off2", 32, U2), ("le", 16, F4), ("lf", 16, F4), ("lid", 16, F4),
+                   ("llr", 16, F4), ("iv", 32, F4), ("ivt", 40, F4), ("ivg", 512, BF), ("inv0", 512, BF), ("idw", 520, F4),
+                   ("g16", 16, F4), ("off3", 16, U2), ("idsel", 64, F4)):
+    SCRATCH[_n] = ("sbuf", [128, _w], _d)
+for _n, _m, _w in (("xq", "xs", 258), ("plq", "pls", 384), ("p2q", "p2s", 384), ("wvq", "wvs", 512), ("wq", "ws", 128), ("send1", "send1s", 512),
+                   ("land1", "land1s", 512), ("ctq", "cts", 512), ("vq", "vs", 512), ("aq", "asc", 512), ("hq", "hs", 514),
+                   ("send2", "send2s", 512), ("land2", "land2s", 512)):
+    SCRATCH[_n] = ("sbuf", [128, _w], CO)
+    SCRATCH[_m] = ("sbuf", [128, _w], PL)
+for _n, _w in (("lst1", 4), ("ldl1", 8), ("lst2", 4), ("ldl2", 8)):
+    SCRATCH[_n] = ("dram", [_w, 128, 1], F4)
 for _h in range(3):
-    SCRATCH["u%d" % _h] = ("sbuf", [128, 768], BF)
-    SCRATCH["k%d" % _h] = ("sbuf", [128, 1024], BF)
-    SCRATCH["z%d" % _h] = ("sbuf", [128, 2048], BF)
-    SCRATCH["zs%d" % _h] = ("sbuf", [128, 2048], BF)
-    SCRATCH["jk%d" % _h] = ("sbuf", [128, 2048], BF)
-    SCRATCH["acc%d" % _h] = ("sbuf", [128, 8], F4)
+    for _n, _w, _d in (("u", 768, BF), ("k", 1024, BF), ("z", 2048, BF), ("zs", 2048, BF), ("jk", 4096, BF), ("acc", 16, F4), ("cn", 16, F4)):
+        SCRATCH["%s%d" % (_n, _h)] = ("sbuf", [128, _w], _d)
 for _h in range(8):
     SCRATCH["ps%d" % _h] = ("psum", [128, 512], F4)
-SEMAPHORES = ["v", "s", "t", "gi", "dx", "dpl", "dwv", "dw", "dp2", "dl1", "dl1o", "dlr", "dl2", "dl2o", "dli", "did",
+SEMAPHORES = ["v", "s", "t", "gi", "dx", "dpl", "dwv", "dw", "dp2", "dl1", "do1", "dlr", "did0", "dl2", "do2", "did",
               "doc", "dy", "snd", "a1", "l1", "a2on", "a2off", "l2"]
 
 
@@ -89,6 +77,12 @@ def rank_program(g, core, T, topo):
             return raised(g.iota(out, pat, base, ch, allow_small_or_imprecise_dtypes=True), "gi", 1)
         return raised(g.iota(out, pat, base, ch), "gi", 1)
 
+    def ts(deps, out, in0, s1, s2, *ops):
+        return v(deps, V.tensor_scalar, out, in0, s1, s2, *ops)
+
+    def cp(deps, out, in_):
+        return v(deps, V.tensor_copy, out, in_)
+
     near = [q for q in range(n_ranks) if topo.chip(cores[q]) == topo.chip(core)]
     far = [q for q in range(n_ranks) if q not in near]
     near_to = [q for q in near if q != r]
@@ -104,35 +98,22 @@ def rank_program(g, core, T, topo):
 
     wf, wn = share(far_pool, len(far)), share(near_pool, len(near_to))
 
-    def send(dests, src, dst, sem_of, codes):
+    def send(src_of, dst_of, sem_of, few):
         tr, tot = [], 0
         used = {"f": 0, "n": 0}
-        for q in dests:
+        for q in far + near_to:
             k, pool, w = ("f", far_pool, wf) if q in far else ("n", near_pool, wn)
+            if few:
+                w = 1
             mask = 0
             for e in pool[used[k]:used[k] + w]:
                 mask += 1 << e
             used[k] += w
             tot += w
             rid, pid, _ = topo.addr(cores[q])
-            a, b = src[:, 64 * q:64 * q + 64], dst[:, 64 * r:64 * r + 64]
-            if codes:
-                a, b = a.bitcast(dt.uint8), b.bitcast(dt.uint8)
-            tr.append(RemoteDMATransfer(dst_ids=[DstId(rid=rid, pnc=pid)], dma_engine_mask=mask, remote_sem=T.sem[sem_of(q)], src=a, dst=b))
+            tr.append(RemoteDMATransfer(dst_ids=[DstId(rid=rid, pnc=pid)], dma_engine_mask=mask, remote_sem=T.sem[sem_of(q)], src=src_of(q), dst=dst_of(q)))
         g.remote_dma_fused(tr, local_sem=T.sem.snd)
         count["snd"] = count.get("snd", 0) + tot
-
-    def send_lists(src_of, dst, sem):
-        tr = []
-        used = {"f": 0, "n": 0}
-        for q in far + near_to:
-            k, pool = ("f", far_pool) if q in far else ("n", near_pool)
-            mask = 1 << pool[used[k]]
-            used[k] += 1
-            rid, pid, _ = topo.addr(cores[q])
-            tr.append(RemoteDMATransfer(dst_ids=[DstId(rid=rid, pnc=pid)], dma_engine_mask=mask, remote_sem=T.sem[sem], src=src_of(q), dst=dst[r]))
-        g.remote_dma_fused(tr, local_sem=T.sem.snd)
-        count["snd"] = count.get("snd", 0) + len(tr)
 
     dpl = dma("s", [], "dpl", T.plin[:, 0:12], T.pl[:, 0:12])
     dx = dma("y", [], "dx", T.xt[:, 0:1024], T.x[:])
@@ -144,20 +125,23 @@ def rank_program(g, core, T, topo):
     i1 = io([[1, 16]], T.i16[:], f32=True)
     i2 = io([[1, 4], [64, 8]], T.ict[:])
     i3 = io([[2, 16], [0, 2]], T.ib[:])
-    i4 = io([[256, 8], [0, 4]], T.cb[:], base=1, f32=True)
+    i4 = io([[0, 16], [-1, 2]], T.ev[:], base=1, f32=True)
     zr = v([], V.memset, T.zr[:], 0.0)
     xz = v([], V.memset, T.xt[:, 1024:1032], 0.0)
-    c1 = v([i0], V.tensor_scalar, T.ii[:, 1:2], T.ii[:, 0:1], 31, 2, op.bitwise_and, op.arith_shift_right)
-    c2 = v([], V.tensor_scalar, T.ii[:, 2:3], T.ii[:, 0:1], 3, None, op.bitwise_and)
-    c3 = v([], V.tensor_scalar, T.ii[:, 3:4], T.ii[:, 0:1], 4, 1, op.arith_shift_right, op.bitwise_and)
-    c4 = v([], V.tensor_scalar, T.ii[:, 4:5], T.ii[:, 0:1], 15, None, op.bitwise_and)
-    dcol = v([c1], V.tensor_scalar, T.dcol[:, 0:1], T.ii[:, 1:2], 8.0, None, op.subtract)
-    m0 = v([c1], V.tensor_scalar, T.cf[:, 2:3], T.ii[:, 1:2], 0.0, None, op.is_equal)
-    f1 = v([c2], V.tensor_scalar, T.cf[:, 1:2], T.ii[:, 2:3], 16.0, None, op.mult)
-    f3 = v([c3], V.tensor_copy, T.cf[:, 3:4], T.ii[:, 3:4])
-    f4 = v([c4], V.tensor_scalar, T.cf[:, 4:5], T.ii[:, 4:5], 4.0, None, op.mult)
-    thr = v([i1, f1], V.tensor_scalar, T.thr[:], T.i16[:], T.cf[:, 1:2], None, op.add)
-    thb = v([i1, f1], V.tensor_scalar, T.thb[:], T.i16[:], T.cf[:, 1:2], 0.5, op.add, op.add)
+    p = T.ii[:, 0:1]
+    c1 = ts([i0], T.ii[:, 1:2], p, 31, 2, op.bitwise_and, op.arith_shift_right)
+    c2 = ts([], T.ii[:, 2:3], p, 3, None, op.bitwise_and)
+    c3 = ts([], T.ii[:, 3:4], p, 4, 1, op.arith_shift_right, op.bitwise_and)
+    c4 = ts([], T.ii[:, 4:5], p, 15, None, op.bitwise_and)
+    c5 = ts([], T.ii[:, 5:6], p, 4, None, op.arith_shift_right)
+    dcol = ts([c1], T.dcol[:, 0:1], T.ii[:, 1:2], 8.0, None, op.subtract)
+    f1 = ts([c2], T.cf[:, 1:2], T.ii[:, 2:3], 16.0, None, op.mult)
+    f3 = cp([c3], T.cf[:, 3:4], T.ii[:, 3:4])
+    f4 = ts([c4], T.cf[:, 4:5], T.ii[:, 4:5], 4.0, None, op.mult)
+    f5 = ts([c4], T.cf[:, 5:6], T.ii[:, 4:5], 4.0, None, op.is_lt)
+    f6 = cp([c2], T.cf[:, 6:7], T.ii[:, 2:3])
+    thr = ts([i1, f1], T.thr[:], T.i16[:], T.cf[:, 1:2], None, op.add)
+    thb = ts([i1, f1], T.thb[:], T.i16[:], T.cf[:, 1:2], 0.5, op.add, op.add)
     r1 = v([], V.memset, T.rp[:], 1.0)
     rp = v([r1], V.memset, T.rp[:, 0:2048:256], 0.0)
 
@@ -168,7 +152,7 @@ def rank_program(g, core, T, topo):
                 k = 4 * b + t
                 o = tile[:, 512 * b + t:512 * b + 512:4]
                 if t < 3:
-                    toks.append(v([din, zr], V.tensor_scalar, o, T.zr[:, 0:128], src[:, k:k + 1], None, op.add))
+                    toks.append(ts([din, zr], o, T.zr[:, 0:128], src[:, k:k + 1], None, op.add))
                 else:
                     toks.append(s([din, zr], o, T.zr[:, 0:128], fn.Identity, bias=src[:, k:k + 1]))
         return v(toks, V.quantize_mx, cod[:], sca[:], tile[:])
@@ -176,85 +160,101 @@ def rank_program(g, core, T, topo):
     plq = planes(dpl, T.plin, T.plt, T.plq, T.pls)
     xq = v([dx, xz], V.quantize_mx, T.xq[:], T.xs[:], T.xt[:])
 
-    def running(h, zt, zp, init, inv, deps):
+    def scan(deps, *a):
+        return v(deps, V.tensor_tensor_scan, *a)
+
+    def running(h, zt, zp, init, inv, deps, between):
         u, k = T["u%d" % h], T["k%d" % h]
-        a = v([zt[0]], V.tensor_scalar, u[:, 0:256], zp[0][:, 0:256], 0.0, -8.0, op.is_lt, op.add)
-        b = v([zt[1]], V.tensor_scalar, u[:, 256:512], zp[1][:, 0:256], 0.0, 2.0, op.is_lt, op.mult)
-        c = v([zt[2]], V.tensor_scalar, u[:, 512:768], zp[2][:, 0:256], 0.0, 4.0, op.is_lt, op.mult)
-        d = v([a, b], V.tensor_tensor_scan, k[:, 0:256], u[:, 256:512], u[:, 0:256], -100.0, op.max, op.add)
-        e = v([c, d], V.tensor_tensor_scan, k[:, 256:512], u[:, 512:768], k[:, 0:256], -100.0, op.max, op.add)
-        f = v([e, dcol], V.tensor_scalar, k[:, 512:768], k[:, 256:512], T.dcol[:, 0:1], None, op.is_equal)
-        return v([f, zr] + deps, V.tensor_tensor_scan, k[:, 768:1024], k[:, 512:768], inv, init, op.add, op.subtract)
+        a, b, c = [ts([zt[i]], u[:, 256 * i:256 * i + 256], zp[i][:, 0:256], 0.0, lo, op.is_lt, m)
+                   for i, (lo, m) in enumerate(((-8.0, op.add), (2.0, op.mult), (4.0, op.mult)))]
+        d = scan([a, b], k[:, 0:256], u[:, 256:512], u[:, 0:256], -100.0, op.max, op.add)
+        between()
+        e = scan([c, d], k[:, 256:512], u[:, 512:768], k[:, 0:256], -100.0, op.max, op.add)
+        between()
+        f = ts([e, dcol], k[:, 512:768], k[:, 256:512], T.dcol[:, 0:1], None, op.is_equal)
+        between()
+        return scan([f, zr] + deps, k[:, 768:1024], k[:, 512:768], inv, init, op.add, op.subtract)
 
-    def counts(h, ct):
-        cc = T["k%d" % h][:, 768:1024]
-        z, zs, jk, acc = T["z%d" % h], T["zs%d" % h], T["jk%d" % h], T["acc%d" % h]
-        st = None
-        for a in range(8):
-            st = s([ct, thb], jk[:, 256 * a:256 * a + 256], cc, fn.Sign, bias=T.thb[:, 8 + a:9 + a], scale=-1.0, accum_out=acc[:, a:a + 1])
-        vt_ = None
-        for a in range(8):
-            vt_ = v([ct, thr], V.tensor_scalar, z[:, 256 * a:256 * a + 256], cc, T.thr[:, a:a + 1], None, op.is_le)
-        return v([vt_, rp], V.tensor_tensor_scan, zs[:], T.rp[:], z[:], 0.0, op.mult, op.add), st
+    def counts_s(h, ct):
+        cc, jk, acc = T["k%d" % h][:, 768:1024], T["jk%d" % h], T["acc%d" % h]
+        x = None
+        for a in range(NV[h], 16):
+            x = s([ct, thb], jk[:, 256 * a:256 * a + 256], cc, fn.Sign, bias=T.thb[:, a:a + 1], scale=-1.0, accum_out=acc[:, a:a + 1])
+        return s([x], T["cn%d" % h][:, NV[h]:16], acc[:, NV[h]:16], fn.Identity, scale=0.5, bias=128.0)
 
-    def offsets(ll, lt, off, deps):
-        a = v(deps, V.transpose, lt[:], ll[:])
-        return v([a], V.tensor_copy, off[:], lt[:])
+    def compare(h, ct, a):
+        return ts([ct, thr], T["z%d" % h][:, 256 * a:256 * a + 256], T["k%d" % h][:, 768:1024], T.thr[:, a:a + 1], None, op.is_le)
+
+    def counts_v(h, ct, a0):
+        z, zs, n = T["z%d" % h], T["zs%d" % h], NV[h]
+        x = None
+        for a in range(a0, n):
+            x = compare(h, ct, a)
+        x = scan([x, rp], zs[:, 0:256 * n], T.rp[:, 0:256 * n], z[:, 0:256 * n], 0.0, op.mult, op.add)
+        return cp([x], T["cn%d" % h][:, 0:n], zs[:, 255:256 * n:256])
 
     zt = [mm([plq, xq], T["ps%d" % b][:, 0:256], T.plq[:, 128 * b:128 * b + 128], T.pls[:, 128 * b:128 * b + 128], T.xq[:, 0:256], T.xs[:, 0:256]) for b in range(3)]
-    ct = running(0, zt, [T.ps0, T.ps1, T.ps2], 0.0, T.zr[:, 0:256], [])
-    cv, cs = counts(0, ct)
-    l1 = s([cs], T.ll1[:, 8:16], T.acc0[:], fn.Identity, scale=0.5, bias=128.0)
-    l2 = s([cs], T.ll1[:, 24:32], T.acc0[:], fn.Identity, scale=0.5, bias=128.0)
-    l3 = v([cv], V.tensor_copy, T.ll1[:, 0:8], T.zs0[:, 255:2048:256])
-    l4 = v([cv], V.tensor_copy, T.ll1[:, 16:24], T.zs0[:, 255:2048:256])
-    o1 = offsets(T.ll1, T.lt1, T.off1, [l1, l2, l3, l4])
-    dl1 = dma("y", [l1, l2, l3, l4], "dl1", T.lst1[:], T.ll1[0:32, 0:32])
-    dl1o = dma("y", [dl1], "dl1o", T.ldl1[r], T.lst1[r])
+    ct = running(0, zt, [T.ps0, T.ps1, T.ps2], 0.0, T.zr[:, 0:256], [], lambda: None)
+    cs = counts_s(0, ct)
+    cv = counts_v(0, ct, 0)
+    l1 = cp([cv, cs], T.ll1[:, 0:16], T.cn0[:])
+    l2 = cp([], T.ll1[:, 16:32], T.cn0[:])
+    le = ts([], T.le[:], T.cn0[:], 255.5, -4096.0, op.is_ge, op.mult)
+    lt = v([l1, l2], V.transpose, T.lt1[:], T.ll1[:])
+    lf = v([le], V.tensor_tensor, T.lf[:], T.cn0[:], T.le[:], op.add)
+    o1 = cp([lt], T.off1[:], T.lt1[:])
+    lid = s([lf], T.lid[:], T.lf[:], fn.Relu, bias=float(256 * r + 1))
 
     def pick(ot, deps, dq, ds, c0, wq_, ws_, wn_, off, e0, n):
         e1 = e0 + n // 16
-        a = v([ot] + deps, V.tensor_copy, dq[:, c0:c0 + n].bitcast(dt.uint32), wq_[:, 0:wn_].bitcast(dt.uint32).indirect(off[:, e0:e1]))
+        a = cp([ot] + deps, dq[:, c0:c0 + n].bitcast(dt.uint32), wq_[:, 0:wn_].bitcast(dt.uint32).indirect(off[:, e0:e1]))
         b = s([ot] + deps, ds[:, c0:c0 + n], ws_[:, 0:wn_].indirect(off[:, e0:e1]), fn.Copy)
         return a, b
 
     def dispatch(ot, deps, sq, ss, lq, ls, wq_, ws_, wn_, off, sem_of):
-        pf = pick(ot, deps, sq, ss, 64 * f0, wq_, ws_, wn_, off, 4 * f0, 64 * len(far))
-        need("g", [pf[0]])
-        send(far, sq, lq, sem_of, True)
-        need("g", [pf[1]])
-        send(far, ss, ls, sem_of, False)
-        pn = pick(ot, deps, sq, ss, 64 * n0, wq_, ws_, wn_, off, 4 * n0, 64 * len(near))
-        need("g", [pn[0]])
-        send(near_to, sq, lq, sem_of, True)
-        need("g", [pn[1]])
-        send(near_to, ss, ls, sem_of, False)
-        return pick(ot, deps, lq, ls, 64 * r, wq_, ws_, wn_, off, 4 * r, 64)
+        pa = pick(ot, deps, sq, ss, 0, wq_, ws_, wn_, off, 0, 64 * n_ranks)
+        need("g", [pa[0]])
+        send(lambda q: sq[:, 64 * q:64 * q + 64].bitcast(dt.uint8), lambda q: lq[:, 64 * r:64 * r + 64].bitcast(dt.uint8), sem_of, False)
+        need("g", [pa[1]])
+        send(lambda q: ss[:, 64 * q:64 * q + 64], lambda q: ls[:, 64 * r:64 * r + 64], sem_of, False)
 
-    own1 = dispatch(o1, [xq], T.send1, T.send1s, T.land1, T.land1s, T.xq, T.xs, 258, T.off1, lambda q: "a1")
+    hf = 64 * (r % 2)
+    dispatch(o1, [xq], T.send1, T.send1s, T.land1, T.land1s, T.xq, T.xs, 258, T.off1, lambda q: "a1")
+    dl1 = dma("y", [lid], "dl1", T.lst1[:], T.lid[0:32, 0:16])
+    do1 = dma("y", [], "do1", T.ldl1[r, hf:hf + 64, 0], T.lid[4 * r:4 * r + 4, 0:16])
+    own1 = pick(o1, [], T.land1, T.land1s, 64 * r, T.xq, T.xs, 258, T.off1, 4 * r, 64)
     need("g", [dl1])
-    send_lists(lambda q: T.lst1[q], T.ldl1, "l1")
+    send(lambda q: T.lst1[q // 2], lambda q: T.ldl1[r], lambda q: "l1", True)
     arr1 = ("a1", 2 * (wf * len(far) + wn * len(near_to)))
     lst1 = ("l1", n_ranks - 1)
     count["a1"], count["l1"] = arr1[1], lst1[1]
 
-    g1 = v([i2, f4], V.tensor_scalar, T.fct[:], T.ict[:], T.cf[:, 4:5], None, op.add)
-    g2 = v([i3, f3], V.tensor_scalar, T.fb[:], T.ib[:], T.cf[:, 3:4], None, op.add)
-    oct_ = v([g1], V.tensor_copy, T.offct[:], T.fct[:])
-    ob = v([g2], V.tensor_copy, T.offb[:], T.fb[:])
+    iz = v([], V.memset, T.idw[:], 0.0)
+    vz = v([], V.memset, T.ivt[:, 32:40], 0.0)
     hz = v([], V.memset, T.ht[:, 2048:2056], 0.0)
-    iz = v([], V.memset, T.idrow[:, 512:520], 0.0)
+    g1 = ts([i2, f4], T.fct[:], T.ict[:], T.cf[:, 4:5], None, op.add)
+    g2 = ts([i3, f3], T.fb[:], T.ib[:], T.cf[:, 3:4], 32.0, op.add, op.subtract)
+    g3 = ts([i4, f5], T.fe[:], T.ev[:], T.cf[:, 5:6], None, op.mult)
+    g5 = ts([c5, f6], T.fg[:, 0:1], T.ii[:, 5:6], 4.0, T.cf[:, 6:7], op.mult, op.add)
+    oct_ = cp([g1], T.offct[:], T.fct[:])
+    g4 = v([g2, g3], V.tensor_tensor, T.fm[:], T.fb[:], T.fe[:], op.mult)
+    og = cp([g5], T.offg[:, 0:1], T.fg[:, 0:1])
+    g6 = ts([g4], T.fo[:], T.fm[:], 32.0, None, op.add)
+    oi = cp([g6], T.offi[:], T.fo[:])
     wvq = v([dwv], V.quantize_mx, T.wvq[:], T.wvs[:], T.wvt[:])
     wq = v([dw], V.quantize_mx, T.wq[:], T.ws[:], T.wt[:])
     p2q = planes(dp2, T.p2in, T.p2t, T.p2q, T.p2s)
 
-    dlr = None
+    dlr = did0 = None
+    mine = T.ldl1[:, hf:hf + 64, 0]
     for a in range(4):
-        dlr = dma("y", [lst1, dl1o], "dlr", T.llr[32 * a:32 * a + 32, 0:32], T.ldl1[:])
+        dlr = dma("y", [lst1, do1], "dlr", T.llr[32 * a:32 * a + 32, 0:16], mine)
+    for a in range(8):
+        did0 = dma("y", [iz], "did0", T.idw[16 * a:16 * a + 1, 0:512], mine)
 
     cpk = []
     for t in range(4):
-        a = v([arr1, oct_, own1[0]], V.tensor_copy, T.ctq[:, 128 * t:128 * t + 128].bitcast(dt.uint32), T.land1[:].bitcast(dt.uint32).indirect(T.offct[:, 8 * t:8 * t + 8]))
+        a = cp([arr1, oct_, own1[0]], T.ctq[:, 128 * t:128 * t + 128].bitcast(dt.uint32), T.land1[:].bitcast(dt.uint32).indirect(T.offct[:, 8 * t:8 * t + 8]))
         b = s([arr1, oct_, own1[1]], T.cts[:, 128 * t:128 * t + 128], T.land1s[:].indirect(T.offct[:, 8 * t:8 * t + 8]), fn.Copy)
         cpk.append([a, b])
 
@@ -266,68 +266,73 @@ def rank_program(g, core, T, topo):
     se = [None] * 4
     for t in range(4):
         o = T.vt[:, t:2048:4]
-        se[t] = s([sm[t]], o, P[t][:], fn.Copy) if t % 2 == 0 else v([sm[t]], V.tensor_copy, o, P[t][:])
+        se[t] = s([sm[t]], o, P[t][:], fn.Copy) if t % 2 == 0 else cp([sm[t]], o, P[t][:])
     vq = v(se, V.quantize_mx, T.vq[:], T.vs[:], T.vt[:])
     aq = []
     for h in range(2):
         rm, re = [], []
         for t in range(4):
-            b = P[(4 if h == 0 else 0) + t]
-            rm.append(mm([own1[0], own1[1], arr1, se[t] if h else None], b[:, 0:256], c_t(t)[0], c_t(t)[1], T.land1[:, 256 * h:256 * h + 256], T.land1s[:, 256 * h:256 * h + 256]))
+            rm.append(mm([own1[0], own1[1], arr1, se[t] if h else None], P[4 - 4 * h + t][:, 0:256], c_t(t)[0], c_t(t)[1],
+                         T.land1[:, 256 * h:256 * h + 256], T.land1s[:, 256 * h:256 * h + 256]))
         for t in range(4):
-            b = P[(4 if h == 0 else 0) + t]
+            b = P[4 - 4 * h + t]
             o = T.at[:, 1024 * h + t:1024 * h + 1024:4]
             if t < 3:
                 re.append(s([rm[t]], o, b[:, 0:256], fn.Relu, scale=0.0625))
             else:
-                re.append(v([rm[t]], V.tensor_scalar, o, b[:, 0:256], 0.0, 0.0625, op.max, op.mult))
+                re.append(ts([rm[t]], o, b[:, 0:256], 0.0, 0.0625, op.max, op.mult))
         aq.append((v(re, V.quantize_mx, T.aq[:, 256 * h:256 * h + 256], T.asc[:, 256 * h:256 * h + 256], T.at[:, 1024 * h:1024 * h + 1024]), re))
-
-    a = v([dlr], V.transpose, T.tr[:], T.llr[:])
-    b = v([a], V.tensor_scalar, T.tv[:], T.tr[:], 255.5, None, op.is_lt)
-    c = v([a, i4], V.tensor_tensor, T.ta[:], T.tr[:], T.cb[:], op.add)
-    d = v([b, c], V.tensor_tensor, T.id1[:], T.tv[:], T.ta[:], op.mult)
-    e = v([d, ob], V.tensor_copy, T.idg[:], T.id1[:].indirect(T.offb[:]))
-    idr = v([e], V.transpose, T.idrow[:, 0:512], T.idg[:])
-    inv = v([idr, m0], V.tensor_scalar, T.inv0[:], T.idrow[:, 0:512], 0.5, T.cf[:, 2:3], op.is_lt, op.mult)
-
-    he, hq = [], []
-    om = []
+    he, hq, om, zt2 = [], [], [], []
     for h in range(2):
-        om.append([mm([vq, aq[h][0]] + aq[h][1], P[(4 if h == 0 else 0) + i][:, 0:256], T.vq[:, 128 * i:128 * i + 128], T.vs[:, 128 * i:128 * i + 128],
+        om.append([mm([vq, aq[h][0]] + aq[h][1], P[4 - 4 * h + i][:, 0:256], T.vq[:, 128 * i:128 * i + 128], T.vs[:, 128 * i:128 * i + 128],
                       T.aq[:, 256 * h:256 * h + 256], T.asc[:, 256 * h:256 * h + 256]) for i in range(4)])
-    zt2 = []
     for h in range(2):
         ev = []
         for i in range(4):
-            b = P[(4 if h == 0 else 0) + i]
-            o = T.ht[:, 1024 * h + i:1024 * h + 1024:4]
-            if h == 0 or i % 2 == 0:
-                ev.append(s([om[h][i]], o, b[:, 0:256], fn.Identity, scale=0.0625))
-            else:
-                ev.append(v([om[h][i]], V.tensor_scalar, o, b[:, 0:256], 0.0625, None, op.mult))
+            ev.append(s([om[h][i]], T.ht[:, 1024 * h + i:1024 * h + 1024:4], P[4 - 4 * h + i][:, 0:256], fn.Identity, scale=0.0625))
         he.append(ev)
         hi = 256 if h == 0 else 514
         hq.append(v(ev + [hz], V.quantize_mx, T.hq[:, 256 * h:hi], T.hs[:, 256 * h:hi], T.ht[:, 1024 * h:4 * hi]))
-        zt2.append([mm([p2q, hq[h]], P[(4 if h == 0 else 0) + b][:, 0:256], T.p2q[:, 128 * b:128 * b + 128], T.p2s[:, 128 * b:128 * b + 128],
+        zt2.append([mm([p2q, hq[h]], P[4 - 4 * h + b][:, 0:256], T.p2q[:, 128 * b:128 * b + 128], T.p2s[:, 128 * b:128 * b + 128],
                        T.hq[:, 256 * h:256 * h + 256], T.hs[:, 256 * h:256 * h + 256]) for b in range(3)])
-    ct1 = running(1, zt2[0], P[4:7], 0.0, T.inv0[:, 0:256], [inv])
-    ct2 = running(2, zt2[1], P[0:3], T.k1[:, 1023:1024], T.inv0[:, 256:512], [inv, ct1])
-    cv1, cs1 = counts(1, ct1)
-    cv2, cs2 = counts(2, ct2)
-    l3 = v([cv1, cv2], V.tensor_tensor, T.ll2[:, 0:8], T.zs1[:, 255:2048:256], T.zs2[:, 255:2048:256], op.add)
-    l4 = v([cv1, cv2], V.tensor_tensor, T.ll2[:, 16:24], T.zs1[:, 255:2048:256], T.zs2[:, 255:2048:256], op.add)
-    sa = v([cs1, cs2], V.tensor_tensor, T.asum[:], T.acc1[:], T.acc2[:], op.add)
-    l1 = v([sa], V.tensor_scalar, T.ll2[:, 8:16], T.asum[:], 0.5, 256.0, op.mult, op.add)
-    l2 = v([sa], V.tensor_scalar, T.ll2[:, 24:32], T.asum[:], 0.5, 256.0, op.mult, op.add)
-    o2 = offsets(T.ll2, T.lt2, T.off2, [l1, l2, l3, l4])
+        if h == 0:
+            a = ts([dlr], T.iv[:, 0:16], T.llr[:], 0.5, None, op.is_lt)
+            b = ts([], T.iv[:, 16:32], T.llr[:], 0.5, None, op.is_lt)
+            iv = v([a, b], V.transpose, T.ivt[:, 0:32], T.iv[:])
+    ivg = s([iv, vz, oi], T.ivg[:], T.ivt[:].indirect(T.offi[:]), fn.Copy)
+    inv = []
 
-    own2 = dispatch(o2, [hq[1]], T.send2, T.send2s, T.land2, T.land2s, T.hq, T.hs, 514, T.off2, lambda q: "a2off" if q in far else "a2on")
-    ids = s([o2, idr, iz], T.idsel[:], T.idrow[:].indirect(T.off2[:]), fn.Copy)
-    dl2 = dma("y", [ids], "dl2", T.lst2[:], T.idsel[0:1, 0:512])
-    dl2o = dma("y", [dl2], "dl2o", T.ldl2[r], T.lst2[r // 2])
+    def turn():
+        if not inv:
+            inv.append(v([ivg], V.transpose, T.inv0[:], T.ivg[:]))
+
+    ct1 = running(1, zt2[0], P[4:7], 0.0, T.inv0[:, 0:256], [], turn)
+    cs1 = counts_s(1, ct1)
+    done = [0]
+
+    def between():
+        if done[0] < NV[1]:
+            compare(1, ct1, done[0])
+            done[0] += 1
+
+    ct2 = running(2, zt2[1], P[0:3], T.k1[:, 1023:1024], T.inv0[:, 256:512], [ct1], between)
+    cv1 = counts_v(1, ct1, done[0])
+    cs2 = counts_s(2, ct2)
+    cv2 = counts_v(2, ct2, 0)
+    l1 = v([cv1, cv2, cs1, cs2], V.tensor_tensor, T.ll2[:, 0:16], T.cn1[:], T.cn2[:], op.add)
+    l2 = v([], V.tensor_tensor, T.ll2[:, 16:32], T.cn1[:], T.cn2[:], op.add)
+    lt = v([l1, l2], V.transpose, T.lt2[:], T.ll2[:])
+    o2 = cp([lt], T.off2[:], T.lt2[:])
+    g16 = cp([og], T.g16[:], T.lt2[:].indirect(T.offg[:, 0:1]))
+
+    dispatch(o2, [hq[1]], T.send2, T.send2s, T.land2, T.land2s, T.hq, T.hs, 514, T.off2, lambda q: "a2off" if q in far else "a2on")
+    o3 = cp([g16], T.off3[:], T.g16[:])
+    ids = ts([o3, did0], T.idsel[:], T.idw[:].indirect(T.off3[:, 0:4]), -1.0, None, op.add)
+    dl2 = dma("y", [ids], "dl2", T.lst2[:], T.idsel[0:128:16, 0:64])
+    do2 = dma("y", [], "do2", T.ldl2[r, hf:hf + 64, 0], T.idsel[16 * r:16 * r + 1, 0:64])
+    own2 = pick(o2, [], T.land2, T.land2s, 64 * r, T.hq, T.hs, 514, T.off2, 4 * r, 64)
     need("g", [dl2])
-    send_lists(lambda q: T.lst2[q // 2], T.ldl2, "l2")
+    send(lambda q: T.lst2[q // 2], lambda q: T.ldl2[r], lambda q: "l2", True)
     an = ("a2on", 2 * wn * len(near_to))
     af = ("a2off", 2 * wf * len(far))
     lst2 = ("l2", n_ranks - 1)
@@ -336,13 +341,11 @@ def rank_program(g, core, T, topo):
     for k, (c0, w, deps) in enumerate(((64 * n0, 64 * len(near), [an, own2[0], own2[1]]), (64 * f0, 64 * len(far), [af]))):
         b = P[7 - 4 * k]
         ym = mm([wq, he[k][3]] + deps, b[:, 0:w], T.wq[:], T.ws[:], T.land2[:, c0:c0 + w], T.land2s[:, c0:c0 + w])
-        ye = v([ym], V.tensor_copy, T.yt[:, c0:c0 + w], b[:, 0:w])
+        ye = cp([ym], T.yt[:, c0:c0 + w], b[:, 0:w])
         dma("s", deps, "doc", T.oc[:, 4 * c0:4 * c0 + 4 * w], T.land2[:, c0:c0 + w].bitcast(dt.uint8))
         if k:
             for m in range(4):
                 dma("s", deps, "doc", T.osc[4 * m:4 * m + 4, :], T.land2s[32 * m:32 * m + 4, :])
         dma("s", [ye], "dy", T.y[:, c0:c0 + w], T.yt[:, c0:c0 + w])
-    dli = dma("y", [lst2, dl2o], "dli", T.idin[:], T.ldl2[:])
-    ido = v([dli], V.tensor_scalar, T.idout[:], T.idin[:, 64 * (r % 2):64 * (r % 2) + 64], -1.0, None, op.add)
-    dma("y", [ido], "did", T.id[:], T.idout[:])
+    dma("y", [lst2, do2], "did", T.id[:], T.ldl2[:, hf:hf + 64, 0])
     need("y", [(k, count[k]) for k in count])

@@ -1,33 +1,37 @@
 from concourse.bass import DstId, RemoteDMATransfer
-from concourse.mybir import dt, AluOpType, ActivationFunctionType
+from concourse.mybir import dt, AluOpType, AxisListType, ActivationFunctionType
 
-NV = [8, 6, 7]
+NV = 8
+RV = (1, 2)
+HV = (2, 2)
+WL, WB = 64, 512
 
 BF, F4, I4, U2, CO, PL = "bfloat16", "float32", "int32", "uint16", "float8_e4m3fn_x4", "uint8"
 SCRATCH = {}
-for _n, _w, _d in (("zr", 256, BF), ("rp", 2048, BF), ("xt", 1032, BF), ("plin", 16, BF), ("plt", 1536, BF), ("p2in", 16, BF),
-                   ("p2t", 1536, BF), ("wvt", 2048, BF), ("wt", 512, BF), ("vt", 2048, BF), ("at", 2048, BF), ("ht", 2056, BF),
-                   ("yt", 512, F4), ("ii", 8, I4), ("ict", 32, I4), ("ib", 32, I4), ("i16", 16, F4), ("ev", 32, F4), ("cf", 8, F4),
-                   ("thr", 16, BF), ("thb", 16, F4), ("dcol", 2, BF), ("fct", 32, F4), ("fb", 32, F4), ("fe", 32, F4), ("fm", 32, F4),
-                   ("fo", 32, F4), ("fg", 2, F4), ("offct", 32, U2), ("offi", 32, U2), ("offg", 2, U2), ("ll1", 32, F4), ("lt1", 32, F4),
-                   ("off1", 32, U2), ("ll2", 32, F4), ("lt2", 32, F4), ("off2", 32, U2), ("le", 16, F4), ("lf", 16, F4), ("lid", 16, F4),
-                   ("llr", 16, F4), ("iv", 32, F4), ("ivt", 40, F4), ("ivg", 512, BF), ("inv0", 512, BF), ("idw", 520, F4),
-                   ("g16", 16, F4), ("off3", 16, U2), ("idsel", 64, F4)):
+for _n, _w, _d in (("zr", 256, BF), ("rp", 2048, BF), ("xt", 1032, BF), ("plt", 512, BF), ("p2t", 512, BF),
+                   ("wvt", 2048, BF), ("wt", 512, BF), ("vt", 2048, BF), ("at", 2048, BF), ("ht", 2056, BF),
+                   ("yt", 512, F4), ("ii", 16, I4), ("fpl", 24, F4), ("offpl", 24, U2), ("i16", 16, F4), ("cf", 16, F4),
+                   ("thr", 16, BF), ("thb", 16, F4), ("dcol", 2, BF), ("dcol2", 2, BF), ("ict", 32, F4), ("fct", 32, F4), ("offct", 32, U2),
+                   ("ip2", 16, F4), ("fp2", 32, F4), ("offp2", 32, U2), ("iu", 32, I4), ("iua", 32, I4), ("iuq", 32, F4), ("iue", 32, F4),
+                   ("iug", 32, F4), ("um", 32, BF), ("itr", 16, F4), ("tri", 16, F4), ("idj", 256, F4), ("dj", 256, F4), ("rp8", 128, BF),
+                   ("fg", 4, F4), ("offg", 2, U2), ("ll1", 32, F4), ("lt1", 32, F4), ("off1", 32, U2), ("off2", 32, U2), ("le", 16, F4),
+                   ("lf", 16, F4), ("lid", 16, F4), ("iv", 128, F4), ("eb", 128, BF), ("et", 128, BF), ("te", 16, F4), ("idw", 520, F4),
+                   ("u1", 768, BF), ("k1", 1024, BF), ("z1", 2048, BF), ("zs1", 2048, BF), ("jk1", 4096, BF), ("acc1", 16, F4), ("cn1", 16, F4),
+                   ("u2", 384, BF), ("k2", 512, BF), ("bc", 32, BF), ("bt", 32, BF), ("og", 2, F4), ("pp", 128, F4), ("pm", 128, F4),
+                   ("pt", 128, F4), ("pc", 128, F4), ("pf", 16, F4), ("pos", 16, U2), ("wn", 8 * WB + 256, F4), ("wtr", 512, F4),
+                   ("lz", 32, F4), ("lzt", 32, F4), ("lx", 64, F4), ("lxt", 64, F4), ("g16", 16, F4), ("off3", 16, U2), ("idsel", 64, F4)):
     SCRATCH[_n] = ("sbuf", [128, _w], _d)
-for _n, _m, _w in (("xq", "xs", 258), ("plq", "pls", 384), ("p2q", "p2s", 384), ("wvq", "wvs", 512), ("wq", "ws", 128), ("send1", "send1s", 512),
-                   ("land1", "land1s", 512), ("ctq", "cts", 512), ("vq", "vs", 512), ("aq", "asc", 512), ("hq", "hs", 514),
-                   ("send2", "send2s", 512), ("land2", "land2s", 512)):
+for _n, _m, _w in (("xq", "xs", 258), ("plr", "plrs", 128), ("plq", "pls", 384), ("p2r", "p2rs", 128), ("p2q", "p2s", 480), ("wvq", "wvs", 512),
+                   ("wq", "ws", 128), ("send1", "send1s", 512), ("land1", "land1s", 512), ("ctq", "cts", 512), ("vq", "vs", 512),
+                   ("aq", "asc", 512), ("hq", "hs", 514), ("send2", "send2s", 512), ("land2", "land2s", 512)):
     SCRATCH[_n] = ("sbuf", [128, _w], CO)
     SCRATCH[_m] = ("sbuf", [128, _w], PL)
 for _n, _w in (("lst1", 4), ("ldl1", 8), ("lst2", 4), ("ldl2", 8)):
     SCRATCH[_n] = ("dram", [_w, 128, 1], F4)
-for _h in range(3):
-    for _n, _w, _d in (("u", 768, BF), ("k", 1024, BF), ("z", 2048, BF), ("zs", 2048, BF), ("jk", 4096, BF), ("acc", 16, F4), ("cn", 16, F4)):
-        SCRATCH["%s%d" % (_n, _h)] = ("sbuf", [128, _w], _d)
 for _h in range(8):
     SCRATCH["ps%d" % _h] = ("psum", [128, 512], F4)
-SEMAPHORES = ["v", "s", "t", "gi", "dx", "dpl", "dwv", "dw", "dp2", "dl1", "do1", "dlr", "did0", "dl2", "do2", "did",
-              "doc", "dy", "snd", "a1", "l1", "a2on", "a2off", "l2"]
+SEMAPHORES = ["v", "s", "t", "gi", "dx", "dpl", "dwv", "dw", "dp2", "dl1", "do1", "div", "did0", "dl2", "do2", "did",
+              "doc", "dos", "dy", "snd", "a1", "l1", "a2on", "a2off", "l2"]
 
 
 def rank_program(g, core, T, topo):
@@ -64,24 +68,36 @@ def rank_program(g, core, T, topo):
         need("s", deps)
         return raised(S.activation(out, in_, func, **k), "s", 1)
 
-    def mm(deps, out, a, asc, b, bsc):
+    def mm(deps, out, a, asc, b, bsc, start=True, stop=True):
         need("t", deps)
-        return raised(PE.matmul_mx(out, a, asc, b, bsc, True, True), "t", 1)
+        return raised(PE.matmul_mx(out, a, asc, b, bsc, start, stop), "t", 1)
 
     def dma(q, deps, sem, out, in_):
         need(q, deps)
         return raised(Q[q].dma_start(out, in_), sem, 16)
 
-    def io(pat, out, base=0, ch=0, f32=False):
-        if f32:
+    def io(pat, out, base=0, ch=0, fl=True):
+        if fl:
             return raised(g.iota(out, pat, base, ch, allow_small_or_imprecise_dtypes=True), "gi", 1)
         return raised(g.iota(out, pat, base, ch), "gi", 1)
 
     def ts(deps, out, in0, s1, s2, *ops):
         return v(deps, V.tensor_scalar, out, in0, s1, s2, *ops)
 
+    def tt(deps, out, a, b, o):
+        return v(deps, V.tensor_tensor, out, a, b, o)
+
     def cp(deps, out, in_):
         return v(deps, V.tensor_copy, out, in_)
+
+    def fill(out, c):
+        return v([], V.memset, out, c)
+
+    def turn(deps, out, in_):
+        return v(deps, V.transpose, out, in_)
+
+    def scan(deps, *a):
+        return v(deps, V.tensor_tensor_scan, *a)
 
     near = [q for q in range(n_ranks) if topo.chip(cores[q]) == topo.chip(core)]
     far = [q for q in range(n_ranks) if q not in near]
@@ -97,158 +113,159 @@ def rank_program(g, core, T, topo):
         return w
 
     wf, wn = share(far_pool, len(far)), share(near_pool, len(near_to))
+    eng = {}
+    for i, q in enumerate(far):
+        eng[q] = far_pool[wf * i:wf * i + wf]
+    for i, q in enumerate(near_to):
+        eng[q] = near_pool[wn * i:wn * i + wn]
 
-    def send(src_of, dst_of, sem_of, few):
-        tr, tot = [], 0
-        used = {"f": 0, "n": 0}
-        for q in far + near_to:
-            k, pool, w = ("f", far_pool, wf) if q in far else ("n", near_pool, wn)
-            if few:
-                w = 1
+    def send(to, src_of, dst_of, sem_of, few=False):
+        tr = []
+        for q in to:
             mask = 0
-            for e in pool[used[k]:used[k] + w]:
+            for e in eng[q][0:1] if few else eng[q]:
                 mask += 1 << e
-            used[k] += w
-            tot += w
+                count["snd"] = count.get("snd", 0) + 1
             rid, pid, _ = topo.addr(cores[q])
             tr.append(RemoteDMATransfer(dst_ids=[DstId(rid=rid, pnc=pid)], dma_engine_mask=mask, remote_sem=T.sem[sem_of(q)], src=src_of(q), dst=dst_of(q)))
         g.remote_dma_fused(tr, local_sem=T.sem.snd)
-        count["snd"] = count.get("snd", 0) + tot
 
-    dpl = dma("s", [], "dpl", T.plin[:, 0:12], T.pl[:, 0:12])
+    dpl = dma("s", [], "dpl", T.plt[:, 0:16], T.pl[:, 0:16])
     dx = dma("y", [], "dx", T.xt[:, 0:1024], T.x[:])
     dwv = dma("y", [dx], "dwv", T.wvt[:], T.wv[:])
     dw = dma("y", [], "dw", T.wt[:], T.w[:])
-    dp2 = dma("y", [], "dp2", T.p2in[:, 0:12], T.p2[:, 0:12])
+    dp2 = dma("y", [], "dp2", T.p2t[:, 0:16], T.p2[:, 0:16])
 
-    i0 = io([[1, 1]], T.ii[:, 0:1], 0, 1)
-    i1 = io([[1, 16]], T.i16[:], f32=True)
+    i0 = io([[1, 1]], T.ii[:, 0:1], 0, 1, False)
+    ip = io([[1, 3], [0, 8]], T.fpl[:])
+    i1 = io([[1, 16]], T.i16[:])
+    ir = io([[0, 2048]], T.rp[:], base=1)
     i2 = io([[1, 4], [64, 8]], T.ict[:])
-    i3 = io([[2, 16], [0, 2]], T.ib[:])
-    i4 = io([[0, 16], [-1, 2]], T.ev[:], base=1, f32=True)
-    zr = v([], V.memset, T.zr[:], 0.0)
-    xz = v([], V.memset, T.xt[:, 1024:1032], 0.0)
+    i3 = io([[-1, 3], [0, 5]], T.ip2[:, 0:15], base=3)
+    i4 = io([[1, 32]], T.iu[:], 128, -1, False)
+    i5 = io([[1, 4], [0, 8]], T.iuq[:])
+    i6 = io([[16, 16]], T.itr[:], base=8 * WB)
+    i7 = io([[32, 4], [128, 4], [1, 16]], T.idj[:], base=-512)
+    pz = fill(T.plt[:, 16:512], 0.0)
+    xz = fill(T.xt[:, 1024:1032], 0.0)
     p = T.ii[:, 0:1]
     c1 = ts([i0], T.ii[:, 1:2], p, 31, 2, op.bitwise_and, op.arith_shift_right)
     c2 = ts([], T.ii[:, 2:3], p, 3, None, op.bitwise_and)
-    c3 = ts([], T.ii[:, 3:4], p, 4, 1, op.arith_shift_right, op.bitwise_and)
-    c4 = ts([], T.ii[:, 4:5], p, 15, None, op.bitwise_and)
-    c5 = ts([], T.ii[:, 5:6], p, 4, None, op.arith_shift_right)
+    opl = cp([ip], T.offpl[:], T.fpl[:])
     dcol = ts([c1], T.dcol[:, 0:1], T.ii[:, 1:2], 8.0, None, op.subtract)
     f1 = ts([c2], T.cf[:, 1:2], T.ii[:, 2:3], 16.0, None, op.mult)
-    f3 = cp([c3], T.cf[:, 3:4], T.ii[:, 3:4])
-    f4 = ts([c4], T.cf[:, 4:5], T.ii[:, 4:5], 4.0, None, op.mult)
-    f5 = ts([c4], T.cf[:, 5:6], T.ii[:, 4:5], 4.0, None, op.is_lt)
-    f6 = cp([c2], T.cf[:, 6:7], T.ii[:, 2:3])
+    zr = fill(T.zr[:], 0.0)
     thr = ts([i1, f1], T.thr[:], T.i16[:], T.cf[:, 1:2], None, op.add)
     thb = ts([i1, f1], T.thb[:], T.i16[:], T.cf[:, 1:2], 0.5, op.add, op.add)
-    r1 = v([], V.memset, T.rp[:], 1.0)
-    rp = v([r1], V.memset, T.rp[:, 0:2048:256], 0.0)
 
-    def planes(din, src, tile, cod, sca):
-        toks = []
-        for b in range(3):
-            for t in range(4):
-                k = 4 * b + t
-                o = tile[:, 512 * b + t:512 * b + 512:4]
-                if t < 3:
-                    toks.append(ts([din, zr], o, T.zr[:, 0:128], src[:, k:k + 1], None, op.add))
-                else:
-                    toks.append(s([din, zr], o, T.zr[:, 0:128], fn.Identity, bias=src[:, k:k + 1]))
-        return v(toks, V.quantize_mx, cod[:], sca[:], tile[:])
+    def pick(deps, dq, ds, c0, wq_, ws_, wn_, off, e0, n):
+        e1 = e0 + n // 16
+        a = cp(deps, dq[:, c0:c0 + n].bitcast(dt.uint32), wq_[:, 0:wn_].bitcast(dt.uint32).indirect(off[:, e0:e1]))
+        b = s(deps, ds[:, c0:c0 + n], ws_[:, 0:wn_].indirect(off[:, e0:e1]), fn.Copy)
+        return [a, b]
 
-    plq = planes(dpl, T.plin, T.plt, T.plq, T.pls)
+    plr = v([dpl, pz], V.quantize_mx, T.plr[:], T.plrs[:], T.plt[:])
+    plq = pick([plr, opl], T.plq, T.pls, 0, T.plr, T.plrs, 128, T.offpl, 0, 384)
     xq = v([dx, xz], V.quantize_mx, T.xq[:], T.xs[:], T.xt[:])
 
-    def scan(deps, *a):
-        return v(deps, V.tensor_tensor_scan, *a)
+    zt = [mm(plq + [xq], T["ps%d" % b][:, 0:256], T.plq[:, 128 * b:128 * b + 128], T.pls[:, 128 * b:128 * b + 128], T.xq[:, 0:256], T.xs[:, 0:256]) for b in range(3)]
 
-    def running(h, zt, zp, init, inv, deps, between):
-        u, k = T["u%d" % h], T["k%d" % h]
-        a, b, c = [ts([zt[i]], u[:, 256 * i:256 * i + 256], zp[i][:, 0:256], 0.0, lo, op.is_lt, m)
+    def number(zt, zp, u, k, w, dc, deps):
+        a, b, c = [ts([zt[i]], u[:, w * i:w * i + w], zp[i][:, 0:w], 0.0, lo, op.is_lt, m)
                    for i, (lo, m) in enumerate(((-8.0, op.add), (2.0, op.mult), (4.0, op.mult)))]
-        d = scan([a, b], k[:, 0:256], u[:, 256:512], u[:, 0:256], -100.0, op.max, op.add)
-        between()
-        e = scan([c, d], k[:, 256:512], u[:, 512:768], k[:, 0:256], -100.0, op.max, op.add)
-        between()
-        f = ts([e, dcol], k[:, 512:768], k[:, 256:512], T.dcol[:, 0:1], None, op.is_equal)
-        between()
-        return scan([f, zr] + deps, k[:, 768:1024], k[:, 512:768], inv, init, op.add, op.subtract)
+        d = scan([a, b], k[:, 0:w], u[:, w:2 * w], u[:, 0:w], -100.0, op.max, op.add)
+        e = scan([c, d], k[:, w:2 * w], u[:, 2 * w:3 * w], k[:, 0:w], -100.0, op.max, op.add)
+        return ts([e] + deps, k[:, 2 * w:3 * w], k[:, w:2 * w], dc, None, op.is_equal)
 
-    def counts_s(h, ct):
-        cc, jk, acc = T["k%d" % h][:, 768:1024], T["jk%d" % h], T["acc%d" % h]
-        x = None
-        for a in range(NV[h], 16):
-            x = s([ct, thb], jk[:, 256 * a:256 * a + 256], cc, fn.Sign, bias=T.thb[:, a:a + 1], scale=-1.0, accum_out=acc[:, a:a + 1])
-        return s([x], T["cn%d" % h][:, NV[h]:16], acc[:, NV[h]:16], fn.Identity, scale=0.5, bias=128.0)
-
-    def compare(h, ct, a):
-        return ts([ct, thr], T["z%d" % h][:, 256 * a:256 * a + 256], T["k%d" % h][:, 768:1024], T.thr[:, a:a + 1], None, op.is_le)
-
-    def counts_v(h, ct, a0):
-        z, zs, n = T["z%d" % h], T["zs%d" % h], NV[h]
-        x = None
-        for a in range(a0, n):
-            x = compare(h, ct, a)
-        x = scan([x, rp], zs[:, 0:256 * n], T.rp[:, 0:256 * n], z[:, 0:256 * n], 0.0, op.mult, op.add)
-        return cp([x], T["cn%d" % h][:, 0:n], zs[:, 255:256 * n:256])
-
-    zt = [mm([plq, xq], T["ps%d" % b][:, 0:256], T.plq[:, 128 * b:128 * b + 128], T.pls[:, 128 * b:128 * b + 128], T.xq[:, 0:256], T.xs[:, 0:256]) for b in range(3)]
-    ct = running(0, zt, [T.ps0, T.ps1, T.ps2], 0.0, T.zr[:, 0:256], [], lambda: None)
-    cs = counts_s(0, ct)
-    cv = counts_v(0, ct, 0)
-    l1 = cp([cv, cs], T.ll1[:, 0:16], T.cn0[:])
-    l2 = cp([], T.ll1[:, 16:32], T.cn0[:])
-    le = ts([], T.le[:], T.cn0[:], 255.5, -4096.0, op.is_ge, op.mult)
-    lt = v([l1, l2], V.transpose, T.lt1[:], T.ll1[:])
-    lf = v([le], V.tensor_tensor, T.lf[:], T.cn0[:], T.le[:], op.add)
+    f = number(zt, [T.ps0, T.ps1, T.ps2], T.u1, T.k1, 256, T.dcol[:, 0:1], [dcol])
+    ct = scan([f, zr], T.k1[:, 768:1024], T.k1[:, 512:768], T.zr[:, 0:256], 0.0, op.add, op.subtract)
+    cc = T.k1[:, 768:1024]
+    x = None
+    for a in range(NV, 16):
+        x = s([ct, thb], T.jk1[:, 256 * a:256 * a + 256], cc, fn.Sign, bias=T.thb[:, a:a + 1], scale=-1.0, accum_out=T.acc1[:, a:a + 1])
+    cs = s([x], T.cn1[:, NV:16], T.acc1[:, NV:16], fn.Identity, scale=0.5, bias=128.0)
+    rp = v([ir], V.memset, T.rp[:, 0:2048:256], 0.0)
+    for a in range(NV):
+        x = ts([ct, thr], T.z1[:, 256 * a:256 * a + 256], cc, T.thr[:, a:a + 1], None, op.is_le)
+    x = scan([x, rp], T.zs1[:, 0:256 * NV], T.rp[:, 0:256 * NV], T.z1[:, 0:256 * NV], 0.0, op.mult, op.add)
+    cv = cp([x], T.cn1[:, 0:NV], T.zs1[:, 255:256 * NV:256])
+    l1 = cp([cv, cs], T.ll1[:, 0:16], T.cn1[:])
+    l2 = cp([], T.ll1[:, 16:32], T.cn1[:])
+    le = ts([], T.le[:], T.cn1[:], 255.5, -4096.0, op.is_ge, op.mult)
+    lt = turn([l1, l2], T.lt1[:], T.ll1[:])
+    lf = tt([le], T.lf[:], T.cn1[:], T.le[:], op.add)
     o1 = cp([lt], T.off1[:], T.lt1[:])
     lid = s([lf], T.lid[:], T.lf[:], fn.Relu, bias=float(256 * r + 1))
 
-    def pick(ot, deps, dq, ds, c0, wq_, ws_, wn_, off, e0, n):
-        e1 = e0 + n // 16
-        a = cp([ot] + deps, dq[:, c0:c0 + n].bitcast(dt.uint32), wq_[:, 0:wn_].bitcast(dt.uint32).indirect(off[:, e0:e1]))
-        b = s([ot] + deps, ds[:, c0:c0 + n], ws_[:, 0:wn_].indirect(off[:, e0:e1]), fn.Copy)
-        return a, b
-
-    def dispatch(ot, deps, sq, ss, lq, ls, wq_, ws_, wn_, off, sem_of):
-        pa = pick(ot, deps, sq, ss, 0, wq_, ws_, wn_, off, 0, 64 * n_ranks)
-        need("g", [pa[0]])
-        send(lambda q: sq[:, 64 * q:64 * q + 64].bitcast(dt.uint8), lambda q: lq[:, 64 * r:64 * r + 64].bitcast(dt.uint8), sem_of, False)
-        need("g", [pa[1]])
-        send(lambda q: ss[:, 64 * q:64 * q + 64], lambda q: ls[:, 64 * r:64 * r + 64], sem_of, False)
+    def dispatch(deps, sq, ss, lq, ls, wq_, ws_, wn_, off, sem_of):
+        pf = pick(deps, sq, ss, 64 * f0, wq_, ws_, wn_, off, 4 * f0, 64 * len(far))
+        need("g", [pf[0]])
+        send(far, lambda q: sq[:, 64 * q:64 * q + 64].bitcast(dt.uint8), lambda q: lq[:, 64 * r:64 * r + 64].bitcast(dt.uint8), sem_of)
+        pn = pick(deps, sq, ss, 64 * n0, wq_, ws_, wn_, off, 4 * n0, 64 * len(near))
+        need("g", [pn[0]])
+        send(near_to, lambda q: sq[:, 64 * q:64 * q + 64].bitcast(dt.uint8), lambda q: lq[:, 64 * r:64 * r + 64].bitcast(dt.uint8), sem_of)
+        need("g", [pf[1], pn[1]])
+        send(far + near_to, lambda q: ss[:, 64 * q:64 * q + 64], lambda q: ls[:, 64 * r:64 * r + 64], sem_of)
 
     hf = 64 * (r % 2)
-    dispatch(o1, [xq], T.send1, T.send1s, T.land1, T.land1s, T.xq, T.xs, 258, T.off1, lambda q: "a1")
     dl1 = dma("y", [lid], "dl1", T.lst1[:], T.lid[0:32, 0:16])
     do1 = dma("y", [], "do1", T.ldl1[r, hf:hf + 64, 0], T.lid[4 * r:4 * r + 4, 0:16])
-    own1 = pick(o1, [], T.land1, T.land1s, 64 * r, T.xq, T.xs, 258, T.off1, 4 * r, 64)
+    dispatch([o1, xq], T.send1, T.send1s, T.land1, T.land1s, T.xq, T.xs, 258, T.off1, lambda q: "a1")
+    own1 = pick([o1, xq], T.land1, T.land1s, 64 * r, T.xq, T.xs, 258, T.off1, 4 * r, 64)
     need("g", [dl1])
-    send(lambda q: T.lst1[q // 2], lambda q: T.ldl1[r], lambda q: "l1", True)
+    send(far + near_to, lambda q: T.lst1[q // 2], lambda q: T.ldl1[r], lambda q: "l1", True)
     arr1 = ("a1", 2 * (wf * len(far) + wn * len(near_to)))
     lst1 = ("l1", n_ranks - 1)
     count["a1"], count["l1"] = arr1[1], lst1[1]
 
-    iz = v([], V.memset, T.idw[:], 0.0)
-    vz = v([], V.memset, T.ivt[:, 32:40], 0.0)
-    hz = v([], V.memset, T.ht[:, 2048:2056], 0.0)
-    g1 = ts([i2, f4], T.fct[:], T.ict[:], T.cf[:, 4:5], None, op.add)
-    g2 = ts([i3, f3], T.fb[:], T.ib[:], T.cf[:, 3:4], 32.0, op.add, op.subtract)
-    g3 = ts([i4, f5], T.fe[:], T.ev[:], T.cf[:, 5:6], None, op.mult)
-    g5 = ts([c5, f6], T.fg[:, 0:1], T.ii[:, 5:6], 4.0, T.cf[:, 6:7], op.mult, op.add)
-    oct_ = cp([g1], T.offct[:], T.fct[:])
-    g4 = v([g2, g3], V.tensor_tensor, T.fm[:], T.fb[:], T.fe[:], op.mult)
-    og = cp([g5], T.offg[:, 0:1], T.fg[:, 0:1])
-    g6 = ts([g4], T.fo[:], T.fm[:], 32.0, None, op.add)
-    oi = cp([g6], T.offi[:], T.fo[:])
+    c4 = ts([], T.ii[:, 4:5], p, 15, None, op.bitwise_and)
+    c3 = ts([], T.ii[:, 3:4], p, 4, 1, op.arith_shift_right, op.bitwise_and)
+    c5 = ts([], T.ii[:, 5:6], p, 4, None, op.arith_shift_right)
+    c6 = ts([], T.ii[:, 6:7], p, 7, None, op.bitwise_and)
+    c7 = ts([], T.ii[:, 7:8], p, 3, 3, op.arith_shift_right, op.bitwise_and)
+    c8 = ts([], T.ii[:, 8:9], p, 1, None, op.bitwise_and)
+    c9 = ts([], T.ii[:, 9:10], p, 1, 1, op.arith_shift_right, op.bitwise_and)
+    ua = ts([i4], T.iua[:], T.iu[:], 7, None, op.bitwise_and)
+    iz = fill(T.idw[:], 0.0)
+    jz = fill(T.iv[:], 1.0)
+    f4 = ts([c4], T.cf[:, 4:5], T.ii[:, 4:5], 4.0, None, op.mult)
+    f3 = ts([c3], T.cf[:, 3:4], T.ii[:, 3:4], 16.0, None, op.mult)
+    f5 = cp([c4], T.cf[:, 5:6], T.ii[:, 4:5])
+    f6 = ts([c4], T.cf[:, 6:7], T.ii[:, 4:5], 8.0, -1.0, op.is_ge, op.mult)
+    f7 = cp([c7], T.cf[:, 7:8], T.ii[:, 7:8])
+    f8 = ts([c6], T.cf[:, 8:9], T.ii[:, 6:7], float(WB), -1.0, op.mult, op.add)
+    f9 = cp([c9], T.cf[:, 9:10], T.ii[:, 9:10])
+    f10 = ts([c8], T.cf[:, 10:11], T.ii[:, 8:9], 32.0, None, op.mult)
+    dcol2 = ts([c6], T.dcol2[:, 0:1], T.ii[:, 6:7], 8.0, None, op.subtract)
+    fct = s([i2, f4], T.fct[:], T.ict[:], fn.Identity, bias=T.cf[:, 4:5])
+    dj = s([i7, f3], T.dj[:], T.idj[:], fn.Identity, bias=T.cf[:, 3:4])
+    tri = s([i6, f5], T.tri[:], T.itr[:], fn.Identity, bias=T.cf[:, 5:6])
+    q3 = fill(T.fp2[:, 0:30], 3.0)
+    ue = ts([ua], T.iue[:], T.iua[:], 0.0, None, op.is_equal)
+    ug = ts([i5, f7], T.iug[:], T.iuq[:], T.cf[:, 7:8], None, op.is_gt)
+    g0 = ts([c5, f9], T.fg[:, 0:1], T.ii[:, 5:6], 2.0, T.cf[:, 9:10], op.mult, op.add)
+    oct_ = cp([fct], T.offct[:], T.fct[:])
     wvq = v([dwv], V.quantize_mx, T.wvq[:], T.wvs[:], T.wvt[:])
+    p2z = fill(T.p2t[:, 16:512], 0.0)
+    hz = fill(T.ht[:, 2048:2056], 0.0)
+    q4 = ts([q3, f6, i3], T.fp2[:, 1:30:2], T.ip2[:, 0:15], T.cf[:, 6:7], 3.0, op.mult, op.add)
+    um = tt([ue, ug], T.um[:], T.iue[:], T.iug[:], op.mult)
+    g1 = ts([g0, f10], T.fg[:, 1:2], T.fg[:, 0:1], T.cf[:, 10:11], None, op.add)
+    op2 = cp([q4], T.offp2[:, 0:30], T.fp2[:, 0:30])
+    p2r = v([dp2, p2z], V.quantize_mx, T.p2r[:], T.p2rs[:], T.p2t[:])
+    r8 = fill(T.rp8[:], 1.0)
+    og = cp([g1], T.offg[:, 0:1], T.fg[:, 1:2])
+    p2q = pick([p2r, op2], T.p2q, T.p2s, 0, T.p2r, T.p2rs, 128, T.offp2, 0, 480)
+    rp8 = v([r8], V.memset, T.rp8[:, 0:128:8], 0.0)
     wq = v([dw], V.quantize_mx, T.wq[:], T.ws[:], T.wt[:])
-    p2q = planes(dp2, T.p2in, T.p2t, T.p2q, T.p2s)
+    for e in range(n_ranks):
+        wz = fill(T.wn[:, WB * e:WB * e + WL], 0.0)
+    lz = fill(T.lz[:], 0.0)
 
-    dlr = did0 = None
+    div = did0 = None
     mine = T.ldl1[:, hf:hf + 64, 0]
     for a in range(4):
-        dlr = dma("y", [lst1, do1], "dlr", T.llr[32 * a:32 * a + 32, 0:16], mine)
+        div = dma("y", [lst1, do1, jz], "div", T.iv[32 * a:32 * a + 32:8, 0:128], mine)
     for a in range(8):
         did0 = dma("y", [iz], "did0", T.idw[16 * a:16 * a + 1, 0:512], mine)
 
@@ -277,75 +294,88 @@ def rank_program(g, core, T, topo):
         for t in range(4):
             b = P[4 - 4 * h + t]
             o = T.at[:, 1024 * h + t:1024 * h + 1024:4]
-            if t < 3:
+            if t < 4 - RV[h]:
                 re.append(s([rm[t]], o, b[:, 0:256], fn.Relu, scale=0.0625))
             else:
                 re.append(ts([rm[t]], o, b[:, 0:256], 0.0, 0.0625, op.max, op.mult))
         aq.append((v(re, V.quantize_mx, T.aq[:, 256 * h:256 * h + 256], T.asc[:, 256 * h:256 * h + 256], T.at[:, 1024 * h:1024 * h + 1024]), re))
-    he, hq, om, zt2 = [], [], [], []
+    om = []
     for h in range(2):
         om.append([mm([vq, aq[h][0]] + aq[h][1], P[4 - 4 * h + i][:, 0:256], T.vq[:, 128 * i:128 * i + 128], T.vs[:, 128 * i:128 * i + 128],
                       T.aq[:, 256 * h:256 * h + 256], T.asc[:, 256 * h:256 * h + 256]) for i in range(4)])
+    ei = s([div], T.eb[:], T.iv[:], fn.Relu, scale=-1.0, bias=1.0)
+    he, hq, zt2 = [], [], [None] * 3
     for h in range(2):
         ev = []
         for i in range(4):
-            ev.append(s([om[h][i]], T.ht[:, 1024 * h + i:1024 * h + 1024:4], P[4 - 4 * h + i][:, 0:256], fn.Identity, scale=0.0625))
+            o, b = T.ht[:, 1024 * h + i:1024 * h + 1024:4], P[4 - 4 * h + i][:, 0:256]
+            if i % 2 == 0 or i >= 2 * HV[h]:
+                ev.append(s([om[h][i]], o, b, fn.Identity, scale=0.0625))
+            else:
+                ev.append(ts([om[h][i]], o, b, 0.0625, None, op.mult))
         he.append(ev)
         hi = 256 if h == 0 else 514
         hq.append(v(ev + [hz], V.quantize_mx, T.hq[:, 256 * h:hi], T.hs[:, 256 * h:hi], T.ht[:, 1024 * h:4 * hi]))
-        zt2.append([mm([p2q, hq[h]], P[4 - 4 * h + b][:, 0:256], T.p2q[:, 128 * b:128 * b + 128], T.p2s[:, 128 * b:128 * b + 128],
-                       T.hq[:, 256 * h:256 * h + 256], T.hs[:, 256 * h:256 * h + 256]) for b in range(3)])
-        if h == 0:
-            a = ts([dlr], T.iv[:, 0:16], T.llr[:], 0.5, None, op.is_lt)
-            b = ts([], T.iv[:, 16:32], T.llr[:], 0.5, None, op.is_lt)
-            iv = v([a, b], V.transpose, T.ivt[:, 0:32], T.iv[:])
-    ivg = s([iv, vz, oi], T.ivg[:], T.ivt[:].indirect(T.offi[:]), fn.Copy)
-    inv = []
+        for b in range(3):
+            for c in (2 * h, 2 * h + 1):
+                w0 = 160 * b + 24 - 8 * c
+                zt2[b] = mm(p2q + [hq[h]] + he[0], P[4 + b][:, 0:128], T.p2q[:, w0:w0 + 128], T.p2s[:, w0:w0 + 128],
+                            T.hq[:, 128 * c:128 * c + 128], T.hs[:, 128 * c:128 * c + 128], c == 0, c == 3)
+    et = turn([ei], T.et[:], T.eb[:])
+    te = tt([et, tri], T.te[:], T.et[:, 0:128:8], T.tri[:], op.mult)
 
-    def turn():
-        if not inv:
-            inv.append(v([ivg], V.transpose, T.inv0[:], T.ivg[:]))
+    f = number(zt2, P[4:7], T.u2, T.k2, 128, T.dcol2[:, 0:1], [dcol2])
+    ff = T.k2[:, 256:384]
+    ct = scan([f, ei], T.k2[:, 384:512], ff, T.eb[:], 0.0, op.add, op.subtract)
+    x = ts([ct, um], T.bc[:], T.um[:], T.k2[:, 511:512], None, op.mult)
+    x = turn([x], T.bt[:], T.bc[:])
+    x = v([x], V.tensor_reduce, T.og[:, 0:1], T.bt[:], AxisListType.X, op.add)
+    x = ts([x, f8], T.pp[:], T.k2[:, 384:512], T.og[:, 0:1], T.cf[:, 8:9], op.add, op.add)
+    x = scan([x, f], T.pm[:], T.pp[:], ff, -100.0, op.max, op.mult)
+    x = turn([x], T.pt[:], T.pm[:])
+    x = scan([x, rp8], T.pc[:], T.rp8[:], T.pt[:], 0.0, op.mult, op.add)
+    x = tt([x, te], T.pf[:], T.pc[:, 7:128:8], T.te[:], op.max)
+    x = cp([x], T.pos[:], T.pf[:])
+    x = cp([x, dj, wz], T.wn[:].indirect(T.pos[:]), T.dj[:])
+    for e in range(n_ranks):
+        y = turn([x], T.wtr[:, WL * e:WL * e + WL], T.wn[:, WB * e:WB * e + WL])
+    x = tt([y, lz], T.lz[:, 0:16], T.wtr[:, 0:512:32], T.wtr[:, 16:512:32], op.add)
+    x = turn([x], T.lzt[:], T.lz[:])
+    xs = [s([x], T.lx[:, 32 * h + 16:32 * h + 32], T.lzt[:, 16 * h:16 * h + 16], fn.Identity, bias=512.0) for h in range(2)]
+    xv = [ts([x], T.lx[:, 32 * h:32 * h + 16], T.lzt[:, 16 * h:16 * h + 16], 512.0, None, op.add) for h in range(2)]
+    x = turn(xs + xv, T.lxt[:], T.lx[:])
+    oa = cp([x], T.off2[:, 0:32:2], T.lxt[:, 0:16])
+    o2 = cp([x], T.off2[:, 1:32:2], T.lxt[:, 32:48])
 
-    ct1 = running(1, zt2[0], P[4:7], 0.0, T.inv0[:, 0:256], [], turn)
-    cs1 = counts_s(1, ct1)
-    done = [0]
-
-    def between():
-        if done[0] < NV[1]:
-            compare(1, ct1, done[0])
-            done[0] += 1
-
-    ct2 = running(2, zt2[1], P[0:3], T.k1[:, 1023:1024], T.inv0[:, 256:512], [ct1], between)
-    cv1 = counts_v(1, ct1, done[0])
-    cs2 = counts_s(2, ct2)
-    cv2 = counts_v(2, ct2, 0)
-    l1 = v([cv1, cv2, cs1, cs2], V.tensor_tensor, T.ll2[:, 0:16], T.cn1[:], T.cn2[:], op.add)
-    l2 = v([], V.tensor_tensor, T.ll2[:, 16:32], T.cn1[:], T.cn2[:], op.add)
-    lt = v([l1, l2], V.transpose, T.lt2[:], T.ll2[:])
-    o2 = cp([lt], T.off2[:], T.lt2[:])
-    g16 = cp([og], T.g16[:], T.lt2[:].indirect(T.offg[:, 0:1]))
-
-    dispatch(o2, [hq[1]], T.send2, T.send2s, T.land2, T.land2s, T.hq, T.hs, 514, T.off2, lambda q: "a2off" if q in far else "a2on")
+    dispatch([oa, o2, hq[1]], T.send2, T.send2s, T.land2, T.land2s, T.hq, T.hs, 514, T.off2, lambda q: "a2off" if q in far else "a2on")
+    g16 = cp([og, x], T.g16[:], T.lxt[:].indirect(T.offg[:, 0:1]))
     o3 = cp([g16], T.off3[:], T.g16[:])
     ids = ts([o3, did0], T.idsel[:], T.idw[:].indirect(T.off3[:, 0:4]), -1.0, None, op.add)
     dl2 = dma("y", [ids], "dl2", T.lst2[:], T.idsel[0:128:16, 0:64])
     do2 = dma("y", [], "do2", T.ldl2[r, hf:hf + 64, 0], T.idsel[16 * r:16 * r + 1, 0:64])
-    own2 = pick(o2, [], T.land2, T.land2s, 64 * r, T.hq, T.hs, 514, T.off2, 4 * r, 64)
+    own2 = pick([o2, hq[1]], T.land2, T.land2s, 64 * r, T.hq, T.hs, 514, T.off2, 4 * r, 64)
     need("g", [dl2])
-    send(lambda q: T.lst2[q // 2], lambda q: T.ldl2[r], lambda q: "l2", True)
+    send(far + near_to, lambda q: T.lst2[q // 2], lambda q: T.ldl2[r], lambda q: "l2", True)
     an = ("a2on", 2 * wn * len(near_to))
     af = ("a2off", 2 * wf * len(far))
     lst2 = ("l2", n_ranks - 1)
     count["a2on"], count["a2off"], count["l2"] = an[1], af[1], lst2[1]
 
-    for k, (c0, w, deps) in enumerate(((64 * n0, 64 * len(near), [an, own2[0], own2[1]]), (64 * f0, 64 * len(far), [af]))):
-        b = P[7 - 4 * k]
-        ym = mm([wq, he[k][3]] + deps, b[:, 0:w], T.wq[:], T.ws[:], T.land2[:, c0:c0 + w], T.land2s[:, c0:c0 + w])
-        ye = cp([ym], T.yt[:, c0:c0 + w], b[:, 0:w])
-        dma("s", deps, "doc", T.oc[:, 4 * c0:4 * c0 + 4 * w], T.land2[:, c0:c0 + w].bitcast(dt.uint8))
-        if k:
-            for m in range(4):
-                dma("s", deps, "doc", T.osc[4 * m:4 * m + 4, :], T.land2s[32 * m:32 * m + 4, :])
-        dma("s", [ye], "dy", T.y[:, c0:c0 + w], T.yt[:, c0:c0 + w])
+    def ycols(b, c0, w, deps):
+        return mm([wq] + deps, b[:, 0:w], T.wq[:], T.ws[:], T.land2[:, c0:c0 + w], T.land2s[:, c0:c0 + w])
+
+    c0, w, dn = 64 * n0, 64 * len(near), [an, own2[0], own2[1]]
+    ym = ycols(P[7], c0, w, he[0] + dn)
+    dma("s", dn, "doc", T.oc[:, 4 * c0:4 * c0 + 4 * w], T.land2[:, c0:c0 + w].bitcast(dt.uint8))
+    ye = cp([ym], T.yt[:, c0:c0 + w], P[7][:, 0:w])
+    dma("s", [ye], "dy", T.y[:, c0:c0 + w], T.yt[:, c0:c0 + w])
+    c0, w = 64 * f0, 64 * len(far)
+    dma("s", [af], "doc", T.oc[:, 4 * c0:4 * c0 + 4 * w], T.land2[:, c0:c0 + w].bitcast(dt.uint8))
+    w //= 2
+    ym = [ycols(P[3 - k], c0 + w * k, w, he[1] + [af]) for k in range(2)]
+    ye = [cp([ym[0]], T.yt[:, c0:c0 + w], P[3][:, 0:w]), s([ym[1]], T.yt[:, c0 + w:c0 + 2 * w], P[2][:, 0:w], fn.Copy)]
+    dma("s", ye, "dy", T.y[:, c0:c0 + 2 * w], T.yt[:, c0:c0 + 2 * w])
+    for m in range(4):
+        dma("y", dn + [af], "dos", T.osc[4 * m:4 * m + 4, :], T.land2s[32 * m:32 * m + 4, :])
     dma("y", [lst2, do2], "did", T.id[:], T.ldl2[:, hf:hf + 64, 0])
     need("y", [(k, count[k]) for k in count])

from concourse.bass import DstId, RemoteDMATransfer
from concourse.mybir import dt, AluOpType, AxisListType, ActivationFunctionType

NV = 8
RV = (1, 2)
HV = (2, 2)
WL, WB = 64, 512

BF, F4, I4, U2, CO, PL = "bfloat16", "float32", "int32", "uint16", "float8_e4m3fn_x4", "uint8"
SCRATCH = {}
for _n, _w, _d in (("zr", 256, BF), ("rp", 2048, BF), ("xt", 1032, BF), ("plt", 512, BF), ("p2t", 512, BF),
                   ("wvt", 2048, BF), ("wt", 512, BF), ("vt", 2048, BF), ("at", 2048, BF), ("ht", 2056, BF),
                   ("yt", 512, F4), ("ii", 16, I4), ("fpl", 24, F4), ("offpl", 24, U2), ("i16", 16, F4), ("cf", 16, F4),
                   ("thr", 16, BF), ("thb", 16, F4), ("dcol", 2, BF), ("dcol2", 2, BF), ("ict", 32, F4), ("fct", 32, F4), ("offct", 32, U2),
                   ("ip2", 16, F4), ("fp2", 32, F4), ("offp2", 32, U2), ("iu", 32, I4), ("iua", 32, I4), ("iuq", 32, F4), ("iue", 32, F4),
                   ("iug", 32, F4), ("um", 32, BF), ("itr", 16, F4), ("tri", 16, F4), ("idj", 256, F4), ("dj", 256, F4), ("rp8", 128, BF),
                   ("fg", 4, F4), ("offg", 2, U2), ("ll1", 32, F4), ("lt1", 32, F4), ("off1", 32, U2), ("off2", 32, U2), ("le", 16, F4),
                   ("lf", 16, F4), ("lid", 16, F4), ("iv", 128, F4), ("eb", 128, BF), ("et", 128, BF), ("te", 16, F4), ("idw", 520, F4),
                   ("u1", 768, BF), ("k1", 1024, BF), ("z1", 2048, BF), ("zs1", 2048, BF), ("jk1", 4096, BF), ("acc1", 16, F4), ("cn1", 16, F4),
                   ("u2", 384, BF), ("k2", 512, BF), ("bc", 32, BF), ("bt", 32, BF), ("og", 2, F4), ("pp", 128, F4), ("pm", 128, F4),
                   ("pt", 128, F4), ("pc", 128, F4), ("pf", 16, F4), ("pos", 16, U2), ("wn", 8 * WB + 256, F4), ("wtr", 512, F4),
                   ("lz", 32, F4), ("lzt", 32, F4), ("lx", 64, F4), ("lxt", 64, F4), ("g16", 16, F4), ("off3", 16, U2), ("idsel", 64, F4)):
    SCRATCH[_n] = ("sbuf", [128, _w], _d)
for _n, _m, _w in (("xq", "xs", 258), ("plr", "plrs", 128), ("plq", "pls", 384), ("p2r", "p2rs", 128), ("p2q", "p2s", 480), ("wvq", "wvs", 512),
                   ("wq", "ws", 128), ("send1", "send1s", 512), ("land1", "land1s", 512), ("ctq", "cts", 512), ("vq", "vs", 512),
                   ("aq", "asc", 512), ("hq", "hs", 514), ("send2", "send2s", 512), ("land2", "land2s", 512)):
    SCRATCH[_n] = ("sbuf", [128, _w], CO)
    SCRATCH[_m] = ("sbuf", [128, _w], PL)
for _n, _w in (("lst1", 4), ("ldl1", 8), ("lst2", 4), ("ldl2", 8)):
    SCRATCH[_n] = ("dram", [_w, 128, 1], F4)
for _h in range(8):
    SCRATCH["ps%d" % _h] = ("psum", [128, 512], F4)
SEMAPHORES = ["v", "s", "t", "gi", "dx", "dpl", "dwv", "dw", "dp2", "dl1", "do1", "div", "did0", "dl2", "do2", "did",
              "doc", "dos", "dy", "snd", "a1", "l1", "a2on", "a2off", "l2"]


def rank_program(g, core, T, topo):
    r = T.rank_of(core)
    if r is None:
        return
    cores = T.cores
    n_ranks = len(cores)
    Q = {"v": g.vector, "s": g.scalar, "t": g.tensor, "y": g.sync, "g": g}
    V, S, PE = g.vector, g.scalar, g.tensor
    op, fn = AluOpType, ActivationFunctionType
    waited, count = {}, {}

    def need(q, deps):
        best = {}
        for d in deps:
            if d is not None:
                best[d[0]] = max(best.get(d[0], 0), d[1])
        for s in best:
            if waited.get((q, s), 0) < best[s]:
                Q[q].wait_ge(T.sem[s], best[s])
                waited[(q, s)] = best[s]

    def raised(ins, s, n):
        ins.then_inc(T.sem[s], n)
        count[s] = count.get(s, 0) + n
        return (s, count[s])

    def v(deps, f, *a):
        need("v", deps)
        return raised(f(*a), "v", 1)

    def s(deps, out, in_, func, **k):
        need("s", deps)
        return raised(S.activation(out, in_, func, **k), "s", 1)

    def mm(deps, out, a, asc, b, bsc, start=True, stop=True):
        need("t", deps)
        return raised(PE.matmul_mx(out, a, asc, b, bsc, start, stop), "t", 1)

    def dma(q, deps, sem, out, in_):
        need(q, deps)
        return raised(Q[q].dma_start(out, in_), sem, 16)

    def io(pat, out, base=0, ch=0, fl=True):
        if fl:
            return raised(g.iota(out, pat, base, ch, allow_small_or_imprecise_dtypes=True), "gi", 1)
        return raised(g.iota(out, pat, base, ch), "gi", 1)

    def ts(deps, out, in0, s1, s2, *ops):
        return v(deps, V.tensor_scalar, out, in0, s1, s2, *ops)

    def tt(deps, out, a, b, o):
        return v(deps, V.tensor_tensor, out, a, b, o)

    def cp(deps, out, in_):
        return v(deps, V.tensor_copy, out, in_)

    def fill(out, c):
        return v([], V.memset, out, c)

    def turn(deps, out, in_):
        return v(deps, V.transpose, out, in_)

    def scan(deps, *a):
        return v(deps, V.tensor_tensor_scan, *a)

    near = [q for q in range(n_ranks) if topo.chip(cores[q]) == topo.chip(core)]
    far = [q for q in range(n_ranks) if q not in near]
    near_to = [q for q in near if q != r]
    n0, f0 = min(near), min(far)
    far_pool = topo.engines(core, cores[far[0]])
    near_pool = [e for e in topo.engines(core, cores[near_to[0]]) if e not in far_pool]

    def share(pool, k):
        w = 1
        while 2 * w * k <= len(pool):
            w *= 2
        return w

    wf, wn = share(far_pool, len(far)), share(near_pool, len(near_to))
    eng = {}
    for i, q in enumerate(far):
        eng[q] = far_pool[wf * i:wf * i + wf]
    for i, q in enumerate(near_to):
        eng[q] = near_pool[wn * i:wn * i + wn]

    def send(to, src_of, dst_of, sem_of, few=False):
        tr = []
        for q in to:
            mask = 0
            for e in eng[q][0:1] if few else eng[q]:
                mask += 1 << e
                count["snd"] = count.get("snd", 0) + 1
            rid, pid, _ = topo.addr(cores[q])
            tr.append(RemoteDMATransfer(dst_ids=[DstId(rid=rid, pnc=pid)], dma_engine_mask=mask, remote_sem=T.sem[sem_of(q)], src=src_of(q), dst=dst_of(q)))
        g.remote_dma_fused(tr, local_sem=T.sem.snd)

    dpl = dma("s", [], "dpl", T.plt[:, 0:16], T.pl[:, 0:16])
    dx = dma("y", [], "dx", T.xt[:, 0:1024], T.x[:])
    dwv = dma("y", [dx], "dwv", T.wvt[:], T.wv[:])
    dw = dma("y", [], "dw", T.wt[:], T.w[:])
    dp2 = dma("y", [], "dp2", T.p2t[:, 0:16], T.p2[:, 0:16])

    i0 = io([[1, 1]], T.ii[:, 0:1], 0, 1, False)
    ip = io([[1, 3], [0, 8]], T.fpl[:])
    i1 = io([[1, 16]], T.i16[:])
    ir = io([[0, 2048]], T.rp[:], base=1)
    i2 = io([[1, 4], [64, 8]], T.ict[:])
    i3 = io([[-1, 3], [0, 5]], T.ip2[:, 0:15], base=3)
    i4 = io([[1, 32]], T.iu[:], 128, -1, False)
    i5 = io([[1, 4], [0, 8]], T.iuq[:])
    i6 = io([[16, 16]], T.itr[:], base=8 * WB)
    i7 = io([[32, 4], [128, 4], [1, 16]], T.idj[:], base=-512)
    pz = fill(T.plt[:, 16:512], 0.0)
    xz = fill(T.xt[:, 1024:1032], 0.0)
    p = T.ii[:, 0:1]
    c1 = ts([i0], T.ii[:, 1:2], p, 31, 2, op.bitwise_and, op.arith_shift_right)
    c2 = ts([], T.ii[:, 2:3], p, 3, None, op.bitwise_and)
    opl = cp([ip], T.offpl[:], T.fpl[:])
    dcol = ts([c1], T.dcol[:, 0:1], T.ii[:, 1:2], 8.0, None, op.subtract)
    f1 = ts([c2], T.cf[:, 1:2], T.ii[:, 2:3], 16.0, None, op.mult)
    zr = fill(T.zr[:], 0.0)
    thr = ts([i1, f1], T.thr[:], T.i16[:], T.cf[:, 1:2], None, op.add)
    thb = ts([i1, f1], T.thb[:], T.i16[:], T.cf[:, 1:2], 0.5, op.add, op.add)

    def pick(deps, dq, ds, c0, wq_, ws_, wn_, off, e0, n):
        e1 = e0 + n // 16
        a = cp(deps, dq[:, c0:c0 + n].bitcast(dt.uint32), wq_[:, 0:wn_].bitcast(dt.uint32).indirect(off[:, e0:e1]))
        b = s(deps, ds[:, c0:c0 + n], ws_[:, 0:wn_].indirect(off[:, e0:e1]), fn.Copy)
        return [a, b]

    plr = v([dpl, pz], V.quantize_mx, T.plr[:], T.plrs[:], T.plt[:])
    plq = pick([plr, opl], T.plq, T.pls, 0, T.plr, T.plrs, 128, T.offpl, 0, 384)
    xq = v([dx, xz], V.quantize_mx, T.xq[:], T.xs[:], T.xt[:])

    zt = [mm(plq + [xq], T["ps%d" % b][:, 0:256], T.plq[:, 128 * b:128 * b + 128], T.pls[:, 128 * b:128 * b + 128], T.xq[:, 0:256], T.xs[:, 0:256]) for b in range(3)]

    def number(zt, zp, u, k, w, dc, deps):
        a, b, c = [ts([zt[i]], u[:, w * i:w * i + w], zp[i][:, 0:w], 0.0, lo, op.is_lt, m)
                   for i, (lo, m) in enumerate(((-8.0, op.add), (2.0, op.mult), (4.0, op.mult)))]
        d = scan([a, b], k[:, 0:w], u[:, w:2 * w], u[:, 0:w], -100.0, op.max, op.add)
        e = scan([c, d], k[:, w:2 * w], u[:, 2 * w:3 * w], k[:, 0:w], -100.0, op.max, op.add)
        return ts([e] + deps, k[:, 2 * w:3 * w], k[:, w:2 * w], dc, None, op.is_equal)

    f = number(zt, [T.ps0, T.ps1, T.ps2], T.u1, T.k1, 256, T.dcol[:, 0:1], [dcol])
    ct = scan([f, zr], T.k1[:, 768:1024], T.k1[:, 512:768], T.zr[:, 0:256], 0.0, op.add, op.subtract)
    cc = T.k1[:, 768:1024]
    x = None
    for a in range(NV, 16):
        x = s([ct, thb], T.jk1[:, 256 * a:256 * a + 256], cc, fn.Sign, bias=T.thb[:, a:a + 1], scale=-1.0, accum_out=T.acc1[:, a:a + 1])
    cs = s([x], T.cn1[:, NV:16], T.acc1[:, NV:16], fn.Identity, scale=0.5, bias=128.0)
    rp = v([ir], V.memset, T.rp[:, 0:2048:256], 0.0)
    for a in range(NV):
        x = ts([ct, thr], T.z1[:, 256 * a:256 * a + 256], cc, T.thr[:, a:a + 1], None, op.is_le)
    x = scan([x, rp], T.zs1[:, 0:256 * NV], T.rp[:, 0:256 * NV], T.z1[:, 0:256 * NV], 0.0, op.mult, op.add)
    cv = cp([x], T.cn1[:, 0:NV], T.zs1[:, 255:256 * NV:256])
    l1 = cp([cv, cs], T.ll1[:, 0:16], T.cn1[:])
    l2 = cp([], T.ll1[:, 16:32], T.cn1[:])
    le = ts([], T.le[:], T.cn1[:], 255.5, -4096.0, op.is_ge, op.mult)
    lt = turn([l1, l2], T.lt1[:], T.ll1[:])
    lf = tt([le], T.lf[:], T.cn1[:], T.le[:], op.add)
    o1 = cp([lt], T.off1[:], T.lt1[:])
    lid = s([lf], T.lid[:], T.lf[:], fn.Relu, bias=float(256 * r + 1))

    def dispatch(deps, sq, ss, lq, ls, wq_, ws_, wn_, off, sem_of):
        pf = pick(deps, sq, ss, 64 * f0, wq_, ws_, wn_, off, 4 * f0, 64 * len(far))
        need("g", [pf[0]])
        send(far, lambda q: sq[:, 64 * q:64 * q + 64].bitcast(dt.uint8), lambda q: lq[:, 64 * r:64 * r + 64].bitcast(dt.uint8), sem_of)
        pn = pick(deps, sq, ss, 64 * n0, wq_, ws_, wn_, off, 4 * n0, 64 * len(near))
        need("g", [pn[0]])
        send(near_to, lambda q: sq[:, 64 * q:64 * q + 64].bitcast(dt.uint8), lambda q: lq[:, 64 * r:64 * r + 64].bitcast(dt.uint8), sem_of)
        need("g", [pf[1], pn[1]])
        send(far + near_to, lambda q: ss[:, 64 * q:64 * q + 64], lambda q: ls[:, 64 * r:64 * r + 64], sem_of)

    hf = 64 * (r % 2)
    dl1 = dma("y", [lid], "dl1", T.lst1[:], T.lid[0:32, 0:16])
    do1 = dma("y", [], "do1", T.ldl1[r, hf:hf + 64, 0], T.lid[4 * r:4 * r + 4, 0:16])
    dispatch([o1, xq], T.send1, T.send1s, T.land1, T.land1s, T.xq, T.xs, 258, T.off1, lambda q: "a1")
    own1 = pick([o1, xq], T.land1, T.land1s, 64 * r, T.xq, T.xs, 258, T.off1, 4 * r, 64)
    need("g", [dl1])
    send(far + near_to, lambda q: T.lst1[q // 2], lambda q: T.ldl1[r], lambda q: "l1", True)
    arr1 = ("a1", 2 * (wf * len(far) + wn * len(near_to)))
    lst1 = ("l1", n_ranks - 1)
    count["a1"], count["l1"] = arr1[1], lst1[1]

    c4 = ts([], T.ii[:, 4:5], p, 15, None, op.bitwise_and)
    c3 = ts([], T.ii[:, 3:4], p, 4, 1, op.arith_shift_right, op.bitwise_and)
    c5 = ts([], T.ii[:, 5:6], p, 4, None, op.arith_shift_right)
    c6 = ts([], T.ii[:, 6:7], p, 7, None, op.bitwise_and)
    c7 = ts([], T.ii[:, 7:8], p, 3, 3, op.arith_shift_right, op.bitwise_and)
    c8 = ts([], T.ii[:, 8:9], p, 1, None, op.bitwise_and)
    c9 = ts([], T.ii[:, 9:10], p, 1, 1, op.arith_shift_right, op.bitwise_and)
    ua = ts([i4], T.iua[:], T.iu[:], 7, None, op.bitwise_and)
    iz = fill(T.idw[:], 0.0)
    jz = fill(T.iv[:], 1.0)
    f4 = ts([c4], T.cf[:, 4:5], T.ii[:, 4:5], 4.0, None, op.mult)
    f3 = ts([c3], T.cf[:, 3:4], T.ii[:, 3:4], 16.0, None, op.mult)
    f5 = cp([c4], T.cf[:, 5:6], T.ii[:, 4:5])
    f6 = ts([c4], T.cf[:, 6:7], T.ii[:, 4:5], 8.0, -1.0, op.is_ge, op.mult)
    f7 = cp([c7], T.cf[:, 7:8], T.ii[:, 7:8])
    f8 = ts([c6], T.cf[:, 8:9], T.ii[:, 6:7], float(WB), -1.0, op.mult, op.add)
    f9 = cp([c9], T.cf[:, 9:10], T.ii[:, 9:10])
    f10 = ts([c8], T.cf[:, 10:11], T.ii[:, 8:9], 32.0, None, op.mult)
    dcol2 = ts([c6], T.dcol2[:, 0:1], T.ii[:, 6:7], 8.0, None, op.subtract)
    fct = s([i2, f4], T.fct[:], T.ict[:], fn.Identity, bias=T.cf[:, 4:5])
    dj = s([i7, f3], T.dj[:], T.idj[:], fn.Identity, bias=T.cf[:, 3:4])
    tri = s([i6, f5], T.tri[:], T.itr[:], fn.Identity, bias=T.cf[:, 5:6])
    q3 = fill(T.fp2[:, 0:30], 3.0)
    ue = ts([ua], T.iue[:], T.iua[:], 0.0, None, op.is_equal)
    ug = ts([i5, f7], T.iug[:], T.iuq[:], T.cf[:, 7:8], None, op.is_gt)
    g0 = ts([c5, f9], T.fg[:, 0:1], T.ii[:, 5:6], 2.0, T.cf[:, 9:10], op.mult, op.add)
    oct_ = cp([fct], T.offct[:], T.fct[:])
    wvq = v([dwv], V.quantize_mx, T.wvq[:], T.wvs[:], T.wvt[:])
    p2z = fill(T.p2t[:, 16:512], 0.0)
    hz = fill(T.ht[:, 2048:2056], 0.0)
    q4 = ts([q3, f6, i3], T.fp2[:, 1:30:2], T.ip2[:, 0:15], T.cf[:, 6:7], 3.0, op.mult, op.add)
    um = tt([ue, ug], T.um[:], T.iue[:], T.iug[:], op.mult)
    g1 = ts([g0, f10], T.fg[:, 1:2], T.fg[:, 0:1], T.cf[:, 10:11], None, op.add)
    op2 = cp([q4], T.offp2[:, 0:30], T.fp2[:, 0:30])
    p2r = v([dp2, p2z], V.quantize_mx, T.p2r[:], T.p2rs[:], T.p2t[:])
    r8 = fill(T.rp8[:], 1.0)
    og = cp([g1], T.offg[:, 0:1], T.fg[:, 1:2])
    p2q = pick([p2r, op2], T.p2q, T.p2s, 0, T.p2r, T.p2rs, 128, T.offp2, 0, 480)
    rp8 = v([r8], V.memset, T.rp8[:, 0:128:8], 0.0)
    wq = v([dw], V.quantize_mx, T.wq[:], T.ws[:], T.wt[:])
    for e in range(n_ranks):
        wz = fill(T.wn[:, WB * e:WB * e + WL], 0.0)
    lz = fill(T.lz[:], 0.0)

    div = did0 = None
    mine = T.ldl1[:, hf:hf + 64, 0]
    for a in range(4):
        div = dma("y", [lst1, do1, jz], "div", T.iv[32 * a:32 * a + 32:8, 0:128], mine)
    for a in range(8):
        did0 = dma("y", [iz], "did0", T.idw[16 * a:16 * a + 1, 0:512], mine)

    cpk = []
    for t in range(4):
        a = cp([arr1, oct_, own1[0]], T.ctq[:, 128 * t:128 * t + 128].bitcast(dt.uint32), T.land1[:].bitcast(dt.uint32).indirect(T.offct[:, 8 * t:8 * t + 8]))
        b = s([arr1, oct_, own1[1]], T.cts[:, 128 * t:128 * t + 128], T.land1s[:].indirect(T.offct[:, 8 * t:8 * t + 8]), fn.Copy)
        cpk.append([a, b])

    def c_t(t):
        return T.ctq[:, 128 * t:128 * t + 128], T.cts[:, 128 * t:128 * t + 128]

    P = [T["ps%d" % b] for b in range(8)]
    sm = [mm(cpk[t] + [wvq, arr1], P[t][:], c_t(t)[0], c_t(t)[1], T.wvq[:], T.wvs[:]) for t in range(4)]
    se = [None] * 4
    for t in range(4):
        o = T.vt[:, t:2048:4]
        se[t] = s([sm[t]], o, P[t][:], fn.Copy) if t % 2 == 0 else cp([sm[t]], o, P[t][:])
    vq = v(se, V.quantize_mx, T.vq[:], T.vs[:], T.vt[:])
    aq = []
    for h in range(2):
        rm, re = [], []
        for t in range(4):
            rm.append(mm([own1[0], own1[1], arr1, se[t] if h else None], P[4 - 4 * h + t][:, 0:256], c_t(t)[0], c_t(t)[1],
                         T.land1[:, 256 * h:256 * h + 256], T.land1s[:, 256 * h:256 * h + 256]))
        for t in range(4):
            b = P[4 - 4 * h + t]
            o = T.at[:, 1024 * h + t:1024 * h + 1024:4]
            if t < 4 - RV[h]:
                re.append(s([rm[t]], o, b[:, 0:256], fn.Relu, scale=0.0625))
            else:
                re.append(ts([rm[t]], o, b[:, 0:256], 0.0, 0.0625, op.max, op.mult))
        aq.append((v(re, V.quantize_mx, T.aq[:, 256 * h:256 * h + 256], T.asc[:, 256 * h:256 * h + 256], T.at[:, 1024 * h:1024 * h + 1024]), re))
    om = []
    for h in range(2):
        om.append([mm([vq, aq[h][0]] + aq[h][1], P[4 - 4 * h + i][:, 0:256], T.vq[:, 128 * i:128 * i + 128], T.vs[:, 128 * i:128 * i + 128],
                      T.aq[:, 256 * h:256 * h + 256], T.asc[:, 256 * h:256 * h + 256]) for i in range(4)])
    ei = s([div], T.eb[:], T.iv[:], fn.Relu, scale=-1.0, bias=1.0)
    he, hq, zt2 = [], [], [None] * 3
    for h in range(2):
        ev = []
        for i in range(4):
            o, b = T.ht[:, 1024 * h + i:1024 * h + 1024:4], P[4 - 4 * h + i][:, 0:256]
            if i % 2 == 0 or i >= 2 * HV[h]:
                ev.append(s([om[h][i]], o, b, fn.Identity, scale=0.0625))
            else:
                ev.append(ts([om[h][i]], o, b, 0.0625, None, op.mult))
        he.append(ev)
        hi = 256 if h == 0 else 514
        hq.append(v(ev + [hz], V.quantize_mx, T.hq[:, 256 * h:hi], T.hs[:, 256 * h:hi], T.ht[:, 1024 * h:4 * hi]))
        for b in range(3):
            for c in (2 * h, 2 * h + 1):
                w0 = 160 * b + 24 - 8 * c
                zt2[b] = mm(p2q + [hq[h]] + he[0], P[4 + b][:, 0:128], T.p2q[:, w0:w0 + 128], T.p2s[:, w0:w0 + 128],
                            T.hq[:, 128 * c:128 * c + 128], T.hs[:, 128 * c:128 * c + 128], c == 0, c == 3)
    et = turn([ei], T.et[:], T.eb[:])
    te = tt([et, tri], T.te[:], T.et[:, 0:128:8], T.tri[:], op.mult)

    f = number(zt2, P[4:7], T.u2, T.k2, 128, T.dcol2[:, 0:1], [dcol2])
    ff = T.k2[:, 256:384]
    ct = scan([f, ei], T.k2[:, 384:512], ff, T.eb[:], 0.0, op.add, op.subtract)
    x = ts([ct, um], T.bc[:], T.um[:], T.k2[:, 511:512], None, op.mult)
    x = turn([x], T.bt[:], T.bc[:])
    x = v([x], V.tensor_reduce, T.og[:, 0:1], T.bt[:], AxisListType.X, op.add)
    x = ts([x, f8], T.pp[:], T.k2[:, 384:512], T.og[:, 0:1], T.cf[:, 8:9], op.add, op.add)
    x = scan([x, f], T.pm[:], T.pp[:], ff, -100.0, op.max, op.mult)
    x = turn([x], T.pt[:], T.pm[:])
    x = scan([x, rp8], T.pc[:], T.rp8[:], T.pt[:], 0.0, op.mult, op.add)
    x = tt([x, te], T.pf[:], T.pc[:, 7:128:8], T.te[:], op.max)
    x = cp([x], T.pos[:], T.pf[:])
    x = cp([x, dj, wz], T.wn[:].indirect(T.pos[:]), T.dj[:])
    for e in range(n_ranks):
        y = turn([x], T.wtr[:, WL * e:WL * e + WL], T.wn[:, WB * e:WB * e + WL])
    x = tt([y, lz], T.lz[:, 0:16], T.wtr[:, 0:512:32], T.wtr[:, 16:512:32], op.add)
    x = turn([x], T.lzt[:], T.lz[:])
    xs = [s([x], T.lx[:, 32 * h + 16:32 * h + 32], T.lzt[:, 16 * h:16 * h + 16], fn.Identity, bias=512.0) for h in range(2)]
    xv = [ts([x], T.lx[:, 32 * h:32 * h + 16], T.lzt[:, 16 * h:16 * h + 16], 512.0, None, op.add) for h in range(2)]
    x = turn(xs + xv, T.lxt[:], T.lx[:])
    oa = cp([x], T.off2[:, 0:32:2], T.lxt[:, 0:16])
    o2 = cp([x], T.off2[:, 1:32:2], T.lxt[:, 32:48])

    dispatch([oa, o2, hq[1]], T.send2, T.send2s, T.land2, T.land2s, T.hq, T.hs, 514, T.off2, lambda q: "a2off" if q in far else "a2on")
    g16 = cp([og, x], T.g16[:], T.lxt[:].indirect(T.offg[:, 0:1]))
    o3 = cp([g16], T.off3[:], T.g16[:])
    ids = ts([o3, did0], T.idsel[:], T.idw[:].indirect(T.off3[:, 0:4]), -1.0, None, op.add)
    dl2 = dma("y", [ids], "dl2", T.lst2[:], T.idsel[0:128:16, 0:64])
    do2 = dma("y", [], "do2", T.ldl2[r, hf:hf + 64, 0], T.idsel[16 * r:16 * r + 1, 0:64])
    own2 = pick([o2, hq[1]], T.land2, T.land2s, 64 * r, T.hq, T.hs, 514, T.off2, 4 * r, 64)
    need("g", [dl2])
    send(far + near_to, lambda q: T.lst2[q // 2], lambda q: T.ldl2[r], lambda q: "l2", True)
    an = ("a2on", 2 * wn * len(near_to))
    af = ("a2off", 2 * wf * len(far))
    lst2 = ("l2", n_ranks - 1)
    count["a2on"], count["a2off"], count["l2"] = an[1], af[1], lst2[1]

    def ycols(b, c0, w, deps):
        return mm([wq] + deps, b[:, 0:w], T.wq[:], T.ws[:], T.land2[:, c0:c0 + w], T.land2s[:, c0:c0 + w])

    c0, w, dn = 64 * n0, 64 * len(near), [an, own2[0], own2[1]]
    ym = ycols(P[7], c0, w, he[0] + dn)
    dma("s", dn, "doc", T.oc[:, 4 * c0:4 * c0 + 4 * w], T.land2[:, c0:c0 + w].bitcast(dt.uint8))
    ye = cp([ym], T.yt[:, c0:c0 + w], P[7][:, 0:w])
    dma("s", [ye], "dy", T.y[:, c0:c0 + w], T.yt[:, c0:c0 + w])
    c0, w = 64 * f0, 64 * len(far)
    dma("s", [af], "doc", T.oc[:, 4 * c0:4 * c0 + 4 * w], T.land2[:, c0:c0 + w].bitcast(dt.uint8))
    w //= 2
    ym = [ycols(P[3 - k], c0 + w * k, w, he[1] + [af]) for k in range(2)]
    ye = [cp([ym[0]], T.yt[:, c0:c0 + w], P[3][:, 0:w]), s([ym[1]], T.yt[:, c0 + w:c0 + 2 * w], P[2][:, 0:w], fn.Copy)]
    dma("s", ye, "dy", T.y[:, c0:c0 + 2 * w], T.yt[:, c0:c0 + 2 * w])
    for m in range(4):
        dma("y", dn + [af], "dos", T.osc[4 * m:4 * m + 4, :], T.land2s[32 * m:32 * m + 4, :])
    dma("y", [lst2, do2], "did", T.id[:], T.ldl2[:, hf:hf + 64, 0])
    need("y", [(k, count[k]) for k in count])
